import numpy as np
import ml_dtypes


def mxq(x, axis, fmt="e4m3"):
    dtype, down = {"e4m3": (ml_dtypes.float8_e4m3fn, 7), "e5m2": (ml_dtypes.float8_e5m2, 14)}[fmt]
    v = np.moveaxis(np.asarray(x, np.float32).astype(ml_dtypes.bfloat16).astype(np.float64), axis, -1)
    blocks = v.reshape(v.shape[:-1] + (-1, 32))
    amax = np.abs(blocks).max(-1, keepdims=True)
    byte = np.maximum(np.where(amax > 0, np.frexp(amax)[1] - 1 + 127, 0) - down, 1)
    scale = np.exp2(byte - 127.0)
    codes = (blocks / scale).astype(np.float32).astype(dtype).astype(np.float64)
    return np.moveaxis((codes * scale).reshape(v.shape), -1, axis)


WIDE = False


def mx_kscale(k):
    if not WIDE:
        return np.ones(k)
    levels = np.array([10, -10, 5, -5, 0])
    if k % 512:
        return np.exp2(np.random.permutation(np.resize(levels, k // 32))).repeat(32)
    a = np.empty((k // 512, 16))
    for p in range(k // 512):
        a[p, :8] = np.random.permutation(np.resize(levels, 8))
        for g in range(8):
            far = levels[np.abs(levels - a[p, g]) >= 10]
            a[p, g + 8] = far[np.random.randint(len(far))]
    return np.exp2(a.ravel()).repeat(32)


def f64(x):
    return np.asarray(x).astype(np.float64)


def striped(idx):
    return np.tile(np.asarray(idx).reshape(-1, 16).T, (8, 1)).astype(np.uint16)


def unstriped(offs):
    return offs[:16].T.reshape(-1).astype(np.int64)


E2M1 = np.array([0.0, 0.5, 1.0, 1.5, 2.0, 3.0, 4.0, 6.0, -0.0, -0.5, -1.0, -1.5, -2.0, -3.0, -4.0, -6.0])


def pack_weight(w, fmt):
    k, n = w.shape
    w = f64(np.asarray(w, np.float32).astype(ml_dtypes.bfloat16)).reshape(k // 32, 32, n)
    amax = np.abs(w).max(1)
    if fmt == "e4m3":
        byte = np.frexp(amax)[1] - 1 + 127 - 7
    else:
        mant, ex = np.frexp(amax / 6.0)
        byte = np.where(mant > 0.5, ex, ex - 1) + 127
    byte = np.clip(np.where(amax > 0, byte, 1), 1, 254)
    scaled = (w * np.exp2(127.0 - byte)[:, None, :]).reshape(k, n).astype(np.float32)
    by_word = np.ascontiguousarray(scaled.reshape(k // 512, 128, 4, n).transpose(0, 1, 3, 2))
    if fmt == "e4m3":
        words = by_word.astype(ml_dtypes.float8_e4m3fn).view(np.uint8)
    else:
        c = by_word.astype(ml_dtypes.float4_e2m1fn).view(np.uint8) & 0xF
        words = (c[..., 0::2] | (c[..., 1::2] << 4)).reshape(k // 512, 128, 2 * n)
    return np.ascontiguousarray(words), np.ascontiguousarray(byte.astype(np.uint8).reshape(k // 512, 16, n))


def unpack_weight(words, scales, fmt):
    g, _, n = scales.shape
    words = np.ascontiguousarray(words).reshape(g, 128, n, -1)
    if fmt == "e4m3":
        vals = words.view(ml_dtypes.float8_e4m3fn).astype(np.float64)
    else:
        nib = np.empty((g, 128, n, 4), np.uint8)
        nib[..., 0::2] = words & 0xF
        nib[..., 1::2] = words >> 4
        vals = E2M1[nib]
    vals = vals * np.repeat(np.exp2(scales.astype(np.float64) - 127.0), 8, axis=1)[..., None]
    return vals.transpose(0, 1, 3, 2).reshape(g * 512, n)


B, N, T, D, DV, NQ = 2, 512, 2048, 512, 256, 256
DRAFT = 128


def setup_inputs():
    n = np.random.standard_normal
    seg = T // B
    idx = np.concatenate([b * seg + np.random.permutation(seg)[:N] for b in range(B)])
    s = mx_kscale(D)[:, None]
    u = np.ones(T)
    u[idx] = mx_kscale(B * N)
    r = np.random.uniform(0.5, 2.0, T)
    qp = [pack_weight(x, "e4m3") for x in n((B, D, NQ)) * s * (1.00 / np.sqrt(D))]
    k = n((D, T)) / s
    v = n((DV, T)) / (u * r)
    kp = pack_weight(k, "e4m3")
    when = np.zeros(T)
    when[idx] = np.concatenate([np.concatenate([np.arange(N - DRAFT), N - DRAFT + np.random.randint(0, 16, DRAFT)]) for b in range(B)])
    return {
        "q_words": np.stack([x[0] for x in qp]),
        "q_scales": np.stack([x[1] for x in qp]),
        "k_words": kp[0],
        "k_scales": kp[1],
        "vT": v.astype(np.float32),
        "vs": np.tile(u * r, (128, 1)).astype(np.float32),
        "pos": np.tile(when, (128, 1)).astype(np.float32),
        "qpos": np.random.randint(N - DRAFT, N - DRAFT + 16, (B, NQ, 1)).astype(np.float32),
        "offs": striped(idx),
    }


def reference(q_words, q_scales, k_words, k_scales, vT, vs, pos, qpos, offs):
    idx = unstriped(offs)
    k = unpack_weight(k_words, k_scales, "e4m3")
    v = f64(vT)
    pick = lambda x: x[:, idx].reshape(x.shape[0], B, N).transpose(1, 0, 2)
    q = np.stack([unpack_weight(q_words[b], q_scales[b], "e4m3") for b in range(B)])
    score = q.transpose(0, 2, 1) @ pick(k)
    score = np.where(pick(f64(pos))[:, :1, :] <= f64(qpos), score, -30000.0)
    m = score.max(-1, keepdims=True)
    p = np.exp(score - m)
    total = p.sum(-1, keepdims=True)
    w = p * pick(f64(vs))[:, :1, :]
    y = mxq(w, 2, "e4m3") @ mxq(pick(v).transpose(0, 2, 1), 1, "e4m3")
    y = y / total
    return y

@@ -1,0 +1,289 @@
+from contextlib import ExitStack
+
+import concourse.mybir as mybir
+from concourse.masks import make_identity
+
+B, N, T, D, DV, NQ = 2, 512, 2048, 512, 256, 256
+FLOPS = 2 * B * NQ * N * (D + DV)
+
+F32 = mybir.dt.float32
+BF16 = mybir.dt.bfloat16
+I32 = mybir.dt.int32
+U32 = mybir.dt.uint32
+U16 = mybir.dt.uint16
+U8 = mybir.dt.uint8
+FP8X4 = mybir.dt.float8_e4m3fn_x4
+ALU = mybir.AluOpType
+ACT = mybir.ActivationFunctionType
+AX = mybir.AxisListType
+
+P = 128
+SEG = T // B
+COLS = N // 16
+QT = NQ // P
+LIVE = P - 1
+STRETCH = 2.0**80
+PENALTY = 2.0**50
+
+
+def tile_attend_soft_draft_segb2q256n512t2048_kernel(
+    tc, q_words, q_scales, k_words, k_scales, vT, vs, pos, qpos, offs, out
+):
+    nc = tc.nc
+    with ExitStack() as ctx:
+        held = ctx.enter_context(tc.tile_pool(name="held", bufs=1))
+        psum = ctx.enter_context(tc.psum_pool(name="psum", bufs=2))
+
+        offsets = held.tile([P, B * COLS], U16, name="offsets")
+        kw_pool = held.tile([P, T], U32, name="kw_pool")
+        ks_pool = held.tile([P, T // 4], I32, name="ks_pool")
+        qw = held.tile([P, B, NQ], U32, name="qw", align_bytes=64)
+        qs = held.tile([P, B * NQ // 4], I32, name="qs", align_bytes=64)
+        pos_pool = held.tile([P, T], F32, name="pos_pool")
+        vs_pool = held.tile([P, T], F32, name="vs_pool")
+        qp = held.tile([P, B * QT], F32, name="qp")
+        qbias = held.tile([P, B * QT], F32, name="qbias")
+        v_raw = [[held.tile([P, SEG], F32, name=f"v_raw{b}{f}") for f in range(2)] for b in range(B)]
+        v_pool = [held.tile([P, T], BF16, name=f"v_pool{f}") for f in range(2)]
+        ident = held.tile([P, P], F32, name="ident")
+        warm = held.tile([P, 2], F32, name="warm")
+        negm = [held.tile([P, 1], F32, name=f"negm{i}") for i in range(B * QT)]
+        total = [held.tile([P, QT], F32, name=f"total{b}") for b in range(B)]
+        inv = [held.tile([P, QT], F32, name=f"inv{b}") for b in range(B)]
+
+        nc.vector.memset(ks_pool[:], 0)
+        nc.vector.memset(qs[:], 0)
+        nc.vector.memset(warm[:, 0:1], 0.0)
+        nc.vector.memset(pos_pool[0:LIVE, :], 0.0)
+        make_identity(nc, ident[:])
+        nc.scalar.activation(warm[:, 1:2], warm[:, 0:1], ACT.Exp)
+
+        kw_dram = k_words[0].rearrange("p n t -> p (n t)")
+
+        def load_kw(b):
+            nc.sync.dma_start(
+                kw_pool[:, b * SEG : (b + 1) * SEG].bitcast(I32),
+                kw_dram[:, 4 * b * SEG : 4 * (b + 1) * SEG].bitcast(I32),
+            )
+
+        def load_v(b, f):
+            nc.sync.dma_start(v_raw[b][f][:], vT[f * P : (f + 1) * P, b * SEG : (b + 1) * SEG])
+
+        nc.sync.dma_start(offsets[:], offs)
+        nc.sync.dma_start(pos_pool[LIVE:P, :], pos[0:1, :])
+        load_kw(0)
+        load_v(0, 0)
+        for g in range(4):
+            nc.sync.dma_start(ks_pool[32 * g : 32 * g + 4, :], k_scales[0, 4 * g : 4 * g + 4, :].bitcast(I32))
+        nc.sync.dma_start(qw[:].bitcast(I32), q_words[:, 0].rearrange("b p q t -> p b (q t)").bitcast(I32))
+        for g in range(4):
+            nc.sync.dma_start(
+                qs[32 * g : 32 * g + 4, :].rearrange("p (b c) -> p b c", b=B),
+                q_scales[:, 0, 4 * g : 4 * g + 4, :].rearrange("b f q -> f b q").bitcast(I32),
+            )
+        load_v(0, 1)
+        with nc.allow_non_contiguous_dma(reason="one place a query row"):
+            nc.sync.dma_start(qp[:], qpos.rearrange("b (h p) o -> p (b h o)", p=P))
+        load_kw(1)
+        load_v(1, 0)
+        load_v(1, 1)
+        for b in range(B):
+            nc.sync.dma_start(vs_pool[:, b * SEG : (b + 1) * SEG], vs[:, b * SEG : (b + 1) * SEG])
+
+        def listed(b):
+            return offsets[:, b * COLS : (b + 1) * COLS]
+
+        def window(b):
+            return slice(0, (b + 1) * SEG)
+
+        kw, ks, posb, vcol, vg = {}, {}, {}, {}, {}
+        score, mask, negs, prob, probT, wT, wq, wsc, vq, vsc = {}, {}, {}, {}, {}, {}, {}, {}, {}, {}
+
+        def gather_kw(b):
+            kw[b] = held.tile([P, N], U32, name=f"kw{b}", align_bytes=64)
+            nc.vector.tensor_copy(kw[b][:], kw_pool[:, window(b)].indirect(listed(b)))
+
+        def gather_ks(b):
+            ks[b] = held.tile([P, N], U8, name=f"ks{b}", align_bytes=64)
+            nc.vector.tensor_copy(ks[b][:], ks_pool[:].bitcast(U8)[:, window(b)].indirect(listed(b)))
+
+        def spread_pos(b):
+            row = held.tile([P, N], F32, name=f"pos_row{b}")
+            nc.vector.tensor_copy(row[:], pos_pool[:].indirect(listed(b)))
+            turned = psum.tile([P, 4, P], F32, name="turned", tag="misc")
+            for c in range(4):
+                nc.tensor.transpose(turned[:, c, :], row[:, c * P : (c + 1) * P], ident[:])
+            col = held.tile([P, 4], F32, name=f"pos_col{b}")
+            nc.scalar.copy(col[:], turned[:, :, LIVE])
+            posb[b] = psum.tile([P, N], F32, name="posb", tag="posb")
+            for c in range(4):
+                nc.tensor.transpose(posb[b][:, c * P : (c + 1) * P], col[:, c : c + 1].to_broadcast([P, P]), ident[:])
+
+        def turn_vs(b):
+            row = held.tile([P, N], F32, name=f"vs_row{b}")
+            nc.vector.tensor_copy(row[:], vs_pool[:, window(b)].indirect(listed(b)))
+            turned = psum.tile([P, 4, P], F32, name="turned", tag="misc")
+            for t in range(4):
+                nc.tensor.transpose(turned[:, t, :], row[:, t:N:4], ident[:])
+            vcol[b] = held.tile([P, 4], F32, name=f"vs_col{b}")
+            nc.scalar.copy(vcol[b][:], turned[:, :, LIVE])
+
+        def cast_v(b, f):
+            nc.scalar.activation(v_pool[f][:, b * SEG : (b + 1) * SEG], v_raw[b][f][:], ACT.Copy)
+
+        def gather_v(b, f):
+            vg[b, f] = held.tile([P, 2, P, 2], BF16, name=f"vg{b}{f}")
+            nc.scalar.activation(
+                vg[b, f][:].rearrange("e u s j -> e s u j"), v_pool[f][:, window(b)].indirect(listed(b)), ACT.Copy
+            )
+
+        def turn_v(b):
+            turned = psum.tile([P, 2, 2, P], F32, name="turned", tag="misc")
+            for f in range(2):
+                words = vg[b, f][:].rearrange("e u s j -> e (u s j)").bitcast(F32)
+                for u in range(2):
+                    nc.tensor.transpose(turned[:, f, u, :], words[:, u * P : (u + 1) * P], ident[:])
+            vg[b] = held.tile([P, 4 * DV], BF16, name=f"vt{b}", align_bytes=64)
+            nc.scalar.copy(
+                vg[b][:].bitcast(F32).rearrange("p (f e u) -> p f e u", f=2, u=2),
+                turned[:].rearrange("p f u e -> p f e u"),
+            )
+
+        def quantize_v(b):
+            vq[b] = held.tile([P, DV], U32, name=f"vq{b}", align_bytes=64)
+            vsc[b] = held.tile([P, DV], U8, name=f"vsc{b}", align_bytes=64)
+            nc.vector.quantize_mx(vq[b][:].bitcast(FP8X4), vsc[b][:], vg[b][:])
+
+        def scores(i):
+            b, h = divmod(i, QT)
+            score[i] = psum.tile([P, N], F32, name="score", tag="score")
+            nc.tensor.matmul_mx(
+                score[i][:],
+                lhsT=qw[:, b, h * P : (h + 1) * P].bitcast(FP8X4),
+                lhsT_scale=qs[:].bitcast(U8)[:, i * P : (i + 1) * P],
+                rhs=kw[b][:].bitcast(FP8X4),
+                rhs_scale=ks[b][:],
+                start=True,
+                stop=True,
+            )
+
+        def make_mask(i):
+            mask[i] = held.tile([P, N], F32, name=f"mask{i}")
+            nc.scalar.activation(mask[i][:], posb[i // QT][:], ACT.Relu, bias=qbias[:, i : i + 1], scale=STRETCH)
+
+        def apply_mask(i):
+            negs[i] = held.tile([P, N], F32, name=f"negs{i}")
+            nc.vector.scalar_tensor_tensor(negs[i][:], mask[i][:], PENALTY, score[i][:], ALU.min, ALU.subtract)
+
+        def row_max(i):
+            nc.vector.tensor_reduce(negm[i][:], negs[i][:], AX.X, ALU.min)
+
+        def weigh(i):
+            b, h = divmod(i, QT)
+            prob[i] = held.tile([P, 4, P], F32, name=f"prob{i}")
+            nc.scalar.activation(
+                prob[i][:].rearrange("q t s -> q s t"),
+                negs[i][:].rearrange("q (s t) -> q s t", t=4),
+                ACT.Exp,
+                bias=negm[i][:],
+                scale=-1.0,
+                accum_out=total[b][:, h : h + 1],
+            )
+
+        def turn_p(i):
+            probT[i] = psum.tile([P, 4, P], F32, name="probT", tag="probT")
+            for t in range(4):
+                nc.tensor.transpose(probT[i][:, t, :], prob[i][:, t, :], ident[:])
+
+        def scale_w(i):
+            wT[i] = held.tile([P, P, 4], BF16, name=f"wT{i}", align_bytes=64)
+            nc.vector.tensor_tensor(
+                wT[i][:],
+                probT[i][:].rearrange("s t q -> s q t"),
+                vcol[i // QT][:].unsqueeze(1).to_broadcast([P, P, 4]),
+                ALU.mult,
+            )
+
+        def quantize_w(i):
+            wq[i] = held.tile([P, P], U32, name=f"wq{i}", align_bytes=64)
+            wsc[i] = held.tile([P, P], U8, name=f"wsc{i}", align_bytes=64)
+            nc.vector.quantize_mx(wq[i][:].bitcast(FP8X4), wsc[i][:], wT[i][:].rearrange("s q t -> s (q t)"))
+
+        def finish(i):
+            b, h = divmod(i, QT)
+            acc = psum.tile([P, N], F32, name="acc", tag="posb")
+            nc.tensor.matmul_mx(
+                acc[:, 0:DV],
+                lhsT=wq[i][:].bitcast(FP8X4),
+                lhsT_scale=wsc[i][:],
+                rhs=vq[b][:].bitcast(FP8X4),
+                rhs_scale=vsc[b][:],
+                start=True,
+                stop=True,
+            )
+            y = held.tile([P, DV], F32, name=f"y{i}")
+            if i == B * QT - 1:
+                nc.vector.tensor_scalar(y[:], acc[:, 0:DV], inv[b][:, h : h + 1], None, ALU.mult)
+            else:
+                nc.scalar.activation(y[:], acc[:, 0:DV], ACT.Copy, scale=inv[b][:, h : h + 1])
+            nc.sync.dma_start(out[b, h * P : (h + 1) * P, :], y[:])
+
+        nc.scalar.mul(qbias[:], qp[:], -STRETCH)
+        cast_v(0, 0)
+        spread_pos(0)
+        gather_kw(0)
+        gather_ks(0)
+        gather_v(0, 0)
+        scores(0)
+        scores(1)
+        make_mask(0)
+        make_mask(1)
+        spread_pos(1)
+        cast_v(0, 1)
+        apply_mask(0)
+        apply_mask(1)
+        row_max(0)
+        row_max(1)
+        gather_v(0, 1)
+        weigh(0)
+        weigh(1)
+        gather_kw(1)
+        gather_ks(1)
+        turn_p(0)
+        turn_p(1)
+        make_mask(2)
+        make_mask(3)
+        scores(2)
+        scores(3)
+        turn_v(0)
+        turn_vs(0)
+        cast_v(1, 0)
+        cast_v(1, 1)
+        apply_mask(2)
+        apply_mask(3)
+        row_max(2)
+        row_max(3)
+        weigh(2)
+        weigh(3)
+        gather_v(1, 0)
+        gather_v(1, 1)
+        turn_vs(1)
+        nc.vector.reciprocal(inv[0][:], total[0][:])
+        scale_w(0)
+        quantize_v(0)
+        scale_w(1)
+        turn_p(2)
+        quantize_w(0)
+        turn_p(3)
+        quantize_w(1)
+        turn_v(1)
+        finish(0)
+        finish(1)
+        nc.vector.reciprocal(inv[1][:], total[1][:])
+        scale_w(2)
+        scale_w(3)
+        quantize_v(1)
+        quantize_w(2)
+        quantize_w(3)
+        finish(2)
+        finish(3)

@@ -18,9 +18,12 @@ ACT = mybir.ActivationFunctionType
 AX = mybir.AxisListType
 
 P = 128
+PACK = 4
 SEG = T // B
 COLS = N // 16
 QT = NQ // P
+TILES = B * QT
+CHUNKS = B * N // P
 LIVE = P - 1
 STRETCH = 2.0**80
 PENALTY = 2.0**50
@@ -41,54 +44,66 @@ def tile_attend_soft_draft_segb2q256n512t2048_kernel(
         qs = held.tile([P, B * NQ // 4], I32, name="qs", align_bytes=64)
         pos_pool = held.tile([P, T], F32, name="pos_pool")
         vs_pool = held.tile([P, T], F32, name="vs_pool")
-        qp = held.tile([P, B * QT], F32, name="qp")
-        qbias = held.tile([P, B * QT], F32, name="qbias")
-        v_raw = [[held.tile([P, SEG], F32, name=f"v_raw{b}{f}") for f in range(2)] for b in range(B)]
+        qp = held.tile([P, TILES], F32, name="qp")
+        qbias = held.tile([P, TILES], F32, name="qbias")
+        v_raw = [held.tile([P, T], F32, name=f"v_raw{f}") for f in range(2)]
         v_pool = [held.tile([P, T], BF16, name=f"v_pool{f}") for f in range(2)]
         ident = held.tile([P, P], F32, name="ident")
         warm = held.tile([P, 2], F32, name="warm")
-        negm = [held.tile([P, 1], F32, name=f"negm{i}") for i in range(B * QT)]
-        total = [held.tile([P, QT], F32, name=f"total{b}") for b in range(B)]
-        inv = [held.tile([P, QT], F32, name=f"inv{b}") for b in range(B)]
+        negm = [held.tile([P, 1], F32, name=f"negm{i}") for i in range(TILES)]
+        totals = held.tile([P, TILES], F32, name="totals")
+        invs = held.tile([P, TILES], F32, name="invs")
 
-        nc.vector.memset(ks_pool[:], 0)
-        nc.vector.memset(qs[:], 0)
+        make_identity(nc, ident[:])
+        nc.gpsimd.memset(ks_pool[:], 0)
+        nc.gpsimd.memset(qs[:], 0)
         nc.vector.memset(warm[:, 0:1], 0.0)
         nc.vector.memset(pos_pool[0:LIVE, :], 0.0)
-        make_identity(nc, ident[:])
-        nc.scalar.activation(warm[:, 1:2], warm[:, 0:1], ACT.Exp)
+        nc.vector.memset(vs_pool[0:LIVE, 0:SEG], 0.0)
+        nc.gpsimd.memset(vs_pool[0:LIVE, SEG:T], 0.0)
 
-        kw_dram = k_words[0].rearrange("p n t -> p (n t)")
+        def own(b):
+            return slice(b * SEG, (b + 1) * SEG)
 
         def load_kw(b):
-            nc.sync.dma_start(
-                kw_pool[:, b * SEG : (b + 1) * SEG].bitcast(I32),
-                kw_dram[:, 4 * b * SEG : 4 * (b + 1) * SEG].bitcast(I32),
-            )
+            words = k_words[0].rearrange("p n t -> p (n t)")
+            nc.sync.dma_start(kw_pool[:, own(b)].bitcast(I32), words[:, PACK * b * SEG : PACK * (b + 1) * SEG].bitcast(I32))
 
-        def load_v(b, f):
-            nc.sync.dma_start(v_raw[b][f][:], vT[f * P : (f + 1) * P, b * SEG : (b + 1) * SEG])
+        def load_v(f, cols):
+            nc.sync.dma_start(v_raw[f][:, cols], vT[f * P : (f + 1) * P, cols])
 
-        nc.sync.dma_start(offsets[:], offs)
-        nc.sync.dma_start(pos_pool[LIVE:P, :], pos[0:1, :])
-        load_kw(0)
-        load_v(0, 0)
-        for g in range(4):
+        def load_ks(g):
             nc.sync.dma_start(ks_pool[32 * g : 32 * g + 4, :], k_scales[0, 4 * g : 4 * g + 4, :].bitcast(I32))
-        nc.sync.dma_start(qw[:].bitcast(I32), q_words[:, 0].rearrange("b p q t -> p b (q t)").bitcast(I32))
-        for g in range(4):
+
+        def load_qs(g):
             nc.sync.dma_start(
                 qs[32 * g : 32 * g + 4, :].rearrange("p (b c) -> p b c", b=B),
                 q_scales[:, 0, 4 * g : 4 * g + 4, :].rearrange("b f q -> f b q").bitcast(I32),
             )
-        load_v(0, 1)
+
+        halves = [slice(0, SEG // 2), slice(SEG // 2, SEG)]
+        nc.scalar.dma_start(pos_pool[LIVE:P, :], pos[0:1, :])
+        nc.scalar.dma_start(vs_pool[LIVE:P, :], vs[0:1, :])
         with nc.allow_non_contiguous_dma(reason="one place a query row"):
             nc.sync.dma_start(qp[:], qpos.rearrange("b (h p) o -> p (b h o)", p=P))
+        nc.sync.dma_start(offsets[:], offs)
+        for cols in halves:
+            load_v(0, cols)
+        load_v(1, own(0))
+        load_v(0, own(1))
+        load_ks(0)
+        load_ks(1)
+        load_qs(0)
+        load_kw(0)
+        load_v(1, own(1))
+        nc.sync.dma_start(qw[:].bitcast(I32), q_words[:, 0].rearrange("b p q t -> p b (q t)").bitcast(I32))
+        load_ks(2)
+        load_ks(3)
         load_kw(1)
-        load_v(1, 0)
-        load_v(1, 1)
-        for b in range(B):
-            nc.sync.dma_start(vs_pool[:, b * SEG : (b + 1) * SEG], vs[:, b * SEG : (b + 1) * SEG])
+        for g in range(1, 4):
+            load_qs(g)
+
+        nc.scalar.activation(warm[:, 1:2], warm[:, 0:1], ACT.Exp)
 
         def listed(b):
             return offsets[:, b * COLS : (b + 1) * COLS]
@@ -96,63 +111,60 @@ def tile_attend_soft_draft_segb2q256n512t2048_kernel(
         def window(b):
             return slice(0, (b + 1) * SEG)
 
-        kw, ks, posb, vcol, vg = {}, {}, {}, {}, {}
-        score, mask, negs, prob, probT, wT, wq, wsc, vq, vsc = {}, {}, {}, {}, {}, {}, {}, {}, {}, {}
+        kw, pos_wide, v_listed = {}, {}, {}
+        score, penalty, negs, prob, probT, wT, wq, wsc = {}, {}, {}, {}, {}, {}, {}, {}
+        ks = held.tile([P, B * N], U8, name="ks", align_bytes=64)
+        vt = held.tile([P, B, DV, PACK], BF16, name="vt", align_bytes=64)
+        vq = held.tile([P, B * DV], U32, name="vq", align_bytes=64)
+        vsc = held.tile([P, B * DV], U8, name="vsc", align_bytes=64)
+        w_pair = held.tile([P, QT, P, PACK], BF16, name="w_pair", align_bytes=64)
+
+        def turn_row(pool, name, piece):
+            row = held.tile([P, B * N], F32, name=name + "_row")
+            nc.vector.tensor_copy(row[:], pool[:].indirect(offsets[:]))
+            turned = psum.tile([P, N], F32, name="turned", tag="turned")
+            for j in reversed(range(CHUNKS)):
+                nc.tensor.transpose(turned[:, 2 * j : 2 * j + P], piece(row, j), ident[:])
+            return turned
+
+        def live_columns(turned, name):
+            col = held.tile([P, CHUNKS], F32, name=name + "_col")
+            nc.scalar.copy(col[:], turned[:, LIVE : LIVE + 2 * CHUNKS : 2])
+            return col
+
+        def widen_pos(turned):
+            col = live_columns(turned, "pos")
+            for b in range(B):
+                pos_wide[b] = psum.tile([P, N], F32, name="pos_wide", tag="pos_wide")
+                for c in range(N // P):
+                    j = b * (N // P) + c
+                    nc.tensor.transpose(
+                        pos_wide[b][:, c * P : (c + 1) * P], col[:, j : j + 1].to_broadcast([P, P]), ident[:]
+                    )
 
         def gather_kw(b):
             kw[b] = held.tile([P, N], U32, name=f"kw{b}", align_bytes=64)
             nc.vector.tensor_copy(kw[b][:], kw_pool[:, window(b)].indirect(listed(b)))
 
-        def gather_ks(b):
-            ks[b] = held.tile([P, N], U8, name=f"ks{b}", align_bytes=64)
-            nc.vector.tensor_copy(ks[b][:], ks_pool[:].bitcast(U8)[:, window(b)].indirect(listed(b)))
-
-        def spread_pos(b):
-            row = held.tile([P, N], F32, name=f"pos_row{b}")
-            nc.vector.tensor_copy(row[:], pos_pool[:].indirect(listed(b)))
-            turned = psum.tile([P, 4, P], F32, name="turned", tag="misc")
-            for c in range(4):
-                nc.tensor.transpose(turned[:, c, :], row[:, c * P : (c + 1) * P], ident[:])
-            col = held.tile([P, 4], F32, name=f"pos_col{b}")
-            nc.scalar.copy(col[:], turned[:, :, LIVE])
-            posb[b] = psum.tile([P, N], F32, name="posb", tag="posb")
-            for c in range(4):
-                nc.tensor.transpose(posb[b][:, c * P : (c + 1) * P], col[:, c : c + 1].to_broadcast([P, P]), ident[:])
-
-        def turn_vs(b):
-            row = held.tile([P, N], F32, name=f"vs_row{b}")
-            nc.vector.tensor_copy(row[:], vs_pool[:, window(b)].indirect(listed(b)))
-            turned = psum.tile([P, 4, P], F32, name="turned", tag="misc")
-            for t in range(4):
-                nc.tensor.transpose(turned[:, t, :], row[:, t:N:4], ident[:])
-            vcol[b] = held.tile([P, 4], F32, name=f"vs_col{b}")
-            nc.scalar.copy(vcol[b][:], turned[:, :, LIVE])
-
-        def cast_v(b, f):
-            nc.scalar.activation(v_pool[f][:, b * SEG : (b + 1) * SEG], v_raw[b][f][:], ACT.Copy)
+        def cast_v(f, cols):
+            nc.scalar.activation(v_pool[f][:, cols], v_raw[f][:, cols], ACT.Copy)
 
         def gather_v(b, f):
-            vg[b, f] = held.tile([P, 2, P, 2], BF16, name=f"vg{b}{f}")
+            v_listed[b, f] = held.tile([P, 2, P, 2], BF16, name=f"v_listed{b}{f}")
             nc.scalar.activation(
-                vg[b, f][:].rearrange("e u s j -> e s u j"), v_pool[f][:, window(b)].indirect(listed(b)), ACT.Copy
+                v_listed[b, f][:].rearrange("e u s j -> e s u j"), v_pool[f][:, window(b)].indirect(listed(b)), ACT.Copy
             )
 
-        def turn_v(b):
-            turned = psum.tile([P, 2, 2, P], F32, name="turned", tag="misc")
+        def turn_v(b, tag):
+            turned = psum.tile([P, 2, 2, P], F32, name="turned_v", tag=tag)
             for f in range(2):
-                words = vg[b, f][:].rearrange("e u s j -> e (u s j)").bitcast(F32)
+                pairs = v_listed[b, f][:].rearrange("e u s j -> e (u s j)").bitcast(F32)
                 for u in range(2):
-                    nc.tensor.transpose(turned[:, f, u, :], words[:, u * P : (u + 1) * P], ident[:])
-            vg[b] = held.tile([P, 4 * DV], BF16, name=f"vt{b}", align_bytes=64)
+                    nc.tensor.transpose(turned[:, f, u, :], pairs[:, u * P : (u + 1) * P], ident[:])
             nc.scalar.copy(
-                vg[b][:].bitcast(F32).rearrange("p (f e u) -> p f e u", f=2, u=2),
-                turned[:].rearrange("p f u e -> p f e u"),
+                vt[:, b].rearrange("s e t -> s (e t)").bitcast(F32).rearrange("s (f e u) -> s f e u", f=2, u=2),
+                turned[:].rearrange("s f u e -> s f e u"),
             )
-
-        def quantize_v(b):
-            vq[b] = held.tile([P, DV], U32, name=f"vq{b}", align_bytes=64)
-            vsc[b] = held.tile([P, DV], U8, name=f"vsc{b}", align_bytes=64)
-            nc.vector.quantize_mx(vq[b][:].bitcast(FP8X4), vsc[b][:], vg[b][:])
 
         def scores(i):
             b, h = divmod(i, QT)
@@ -162,128 +174,119 @@ def tile_attend_soft_draft_segb2q256n512t2048_kernel(
                 lhsT=qw[:, b, h * P : (h + 1) * P].bitcast(FP8X4),
                 lhsT_scale=qs[:].bitcast(U8)[:, i * P : (i + 1) * P],
                 rhs=kw[b][:].bitcast(FP8X4),
-                rhs_scale=ks[b][:],
+                rhs_scale=ks[:, b * N : (b + 1) * N],
                 start=True,
                 stop=True,
             )
 
-        def make_mask(i):
-            mask[i] = held.tile([P, N], F32, name=f"mask{i}")
-            nc.scalar.activation(mask[i][:], posb[i // QT][:], ACT.Relu, bias=qbias[:, i : i + 1], scale=STRETCH)
+        def make_penalty(i):
+            penalty[i] = held.tile([P, N], F32, name=f"penalty{i}")
+            nc.scalar.activation(penalty[i][:], pos_wide[i // QT][:], ACT.Relu, bias=qbias[:, i : i + 1], scale=STRETCH)
 
         def apply_mask(i):
             negs[i] = held.tile([P, N], F32, name=f"negs{i}")
-            nc.vector.scalar_tensor_tensor(negs[i][:], mask[i][:], PENALTY, score[i][:], ALU.min, ALU.subtract)
-
-        def row_max(i):
-            nc.vector.tensor_reduce(negm[i][:], negs[i][:], AX.X, ALU.min)
+            nc.vector.scalar_tensor_tensor(negs[i][:], penalty[i][:], PENALTY, score[i][:], ALU.min, ALU.subtract)
 
         def weigh(i):
-            b, h = divmod(i, QT)
-            prob[i] = held.tile([P, 4, P], F32, name=f"prob{i}")
+            nc.vector.tensor_reduce(negm[i][:], negs[i][:], AX.X, ALU.min)
+            prob[i] = held.tile([P, PACK, P], F32, name=f"prob{i}")
             nc.scalar.activation(
                 prob[i][:].rearrange("q t s -> q s t"),
-                negs[i][:].rearrange("q (s t) -> q s t", t=4),
+                negs[i][:].rearrange("q (s t) -> q s t", t=PACK),
                 ACT.Exp,
                 bias=negm[i][:],
                 scale=-1.0,
-                accum_out=total[b][:, h : h + 1],
+                accum_out=totals[:, i : i + 1],
             )
 
-        def turn_p(i):
-            probT[i] = psum.tile([P, 4, P], F32, name="probT", tag="probT")
-            for t in range(4):
+        def turn_p(i, tag):
+            probT[i] = psum.tile([P, PACK, P], F32, name="probT", tag=tag)
+            for t in range(PACK):
                 nc.tensor.transpose(probT[i][:, t, :], prob[i][:, t, :], ident[:])
 
-        def scale_w(i):
-            wT[i] = held.tile([P, P, 4], BF16, name=f"wT{i}", align_bytes=64)
+        def scale_w(i, vs_col):
+            b = i // QT
+            wT[i] = w_pair[:, i] if b == 0 else held.tile([P, P, PACK], BF16, name=f"wT{i}", align_bytes=64)
             nc.vector.tensor_tensor(
                 wT[i][:],
                 probT[i][:].rearrange("s t q -> s q t"),
-                vcol[i // QT][:].unsqueeze(1).to_broadcast([P, P, 4]),
+                vs_col[:, PACK * b : PACK * (b + 1)].unsqueeze(1).to_broadcast([P, P, PACK]),
                 ALU.mult,
             )
 
-        def quantize_w(i):
-            wq[i] = held.tile([P, P], U32, name=f"wq{i}", align_bytes=64)
-            wsc[i] = held.tile([P, P], U8, name=f"wsc{i}", align_bytes=64)
-            nc.vector.quantize_mx(wq[i][:].bitcast(FP8X4), wsc[i][:], wT[i][:].rearrange("s q t -> s (q t)"))
+        def quantize_w(tiles, values):
+            codes = held.tile([P, len(tiles) * P], U32, name=f"wq{tiles[0]}", align_bytes=64)
+            scales = held.tile([P, len(tiles) * P], U8, name=f"wsc{tiles[0]}", align_bytes=64)
+            nc.vector.quantize_mx(codes[:].bitcast(FP8X4), scales[:], values)
+            for n, i in enumerate(tiles):
+                wq[i] = codes[:, n * P : (n + 1) * P]
+                wsc[i] = scales[:, n * P : (n + 1) * P]
 
-        def finish(i):
+        def finish(i, tag):
             b, h = divmod(i, QT)
-            acc = psum.tile([P, N], F32, name="acc", tag="posb")
+            acc = psum.tile([P, N], F32, name="acc", tag=tag)
             nc.tensor.matmul_mx(
                 acc[:, 0:DV],
-                lhsT=wq[i][:].bitcast(FP8X4),
-                lhsT_scale=wsc[i][:],
-                rhs=vq[b][:].bitcast(FP8X4),
-                rhs_scale=vsc[b][:],
+                lhsT=wq[i].bitcast(FP8X4),
+                lhsT_scale=wsc[i],
+                rhs=vq[:, b * DV : (b + 1) * DV].bitcast(FP8X4),
+                rhs_scale=vsc[:, b * DV : (b + 1) * DV],
                 start=True,
                 stop=True,
             )
             y = held.tile([P, DV], F32, name=f"y{i}")
-            if i == B * QT - 1:
-                nc.vector.tensor_scalar(y[:], acc[:, 0:DV], inv[b][:, h : h + 1], None, ALU.mult)
+            if i == TILES - 1:
+                nc.vector.tensor_scalar(y[:], acc[:, 0:DV], invs[:, i : i + 1], None, ALU.mult)
             else:
-                nc.scalar.activation(y[:], acc[:, 0:DV], ACT.Copy, scale=inv[b][:, h : h + 1])
+                nc.scalar.activation(y[:], acc[:, 0:DV], ACT.Copy, scale=invs[:, i : i + 1])
             nc.sync.dma_start(out[b, h * P : (h + 1) * P, :], y[:])
 
+        pos_turned = turn_row(pos_pool, "pos", lambda row, j: row[:, j * P : (j + 1) * P])
+        for cols in halves:
+            cast_v(0, cols)
         nc.scalar.mul(qbias[:], qp[:], -STRETCH)
-        cast_v(0, 0)
-        spread_pos(0)
-        gather_kw(0)
-        gather_ks(0)
         gather_v(0, 0)
-        scores(0)
-        scores(1)
-        make_mask(0)
-        make_mask(1)
-        spread_pos(1)
-        cast_v(0, 1)
-        apply_mask(0)
-        apply_mask(1)
-        row_max(0)
-        row_max(1)
+        cast_v(1, own(0))
+        widen_pos(pos_turned)
         gather_v(0, 1)
-        weigh(0)
-        weigh(1)
-        gather_kw(1)
-        gather_ks(1)
-        turn_p(0)
-        turn_p(1)
-        make_mask(2)
-        make_mask(3)
-        scores(2)
-        scores(3)
-        turn_v(0)
-        turn_vs(0)
-        cast_v(1, 0)
-        cast_v(1, 1)
-        apply_mask(2)
-        apply_mask(3)
-        row_max(2)
-        row_max(3)
+        nc.vector.tensor_copy(ks[:], ks_pool[:].bitcast(U8).indirect(offsets[:]))
+        for b in range(B):
+            gather_kw(b)
+        nc.vector.tensor_copy(v_pool[1][:, own(1)], v_raw[1][:, own(1)])
+        cast_v(0, own(1))
+        for i in range(TILES):
+            make_penalty(i)
+
+        for i in range(QT):
+            scores(i)
+        for i in range(QT):
+            apply_mask(i)
+        for f in range(2):
+            gather_v(1, f)
+        for i in range(QT, TILES):
+            scores(i)
+        for i in range(QT):
+            weigh(i)
+            apply_mask(i + QT)
+        turn_v(0, "turned")
+        turn_p(0, "probT")
         weigh(2)
+        vs_turned = turn_row(vs_pool, "vs", lambda row, j: row[:, (j // PACK) * N + j % PACK : (j // PACK + 1) * N : PACK])
+        vs_col = live_columns(vs_turned, "vs")
         weigh(3)
-        gather_v(1, 0)
-        gather_v(1, 1)
-        turn_vs(1)
-        nc.vector.reciprocal(inv[0][:], total[0][:])
-        scale_w(0)
-        quantize_v(0)
-        scale_w(1)
-        turn_p(2)
-        quantize_w(0)
-        turn_p(3)
-        quantize_w(1)
-        turn_v(1)
-        finish(0)
-        finish(1)
-        nc.vector.reciprocal(inv[1][:], total[1][:])
-        scale_w(2)
-        scale_w(3)
-        quantize_v(1)
-        quantize_w(2)
-        quantize_w(3)
-        finish(2)
-        finish(3)
+        turn_v(1, "score")
+        turn_p(1, "probT")
+        for i in range(QT, TILES):
+            turn_p(i, "turned")
+
+        scale_w(0, vs_col)
+        nc.vector.quantize_mx(vq[:].bitcast(FP8X4), vsc[:], vt[:].rearrange("s b e t -> s (b e t)"))
+        scale_w(1, vs_col)
+        nc.vector.reciprocal(invs[:], totals[:])
+        scale_w(2, vs_col)
+        quantize_w([0, 1], w_pair[:].rearrange("s i q t -> s (i q t)"))
+        scale_w(3, vs_col)
+        for i in range(QT, TILES):
+            quantize_w([i], wT[i][:].rearrange("s q t -> s (q t)"))
+        for i in range(TILES):
+            finish(i, "pos_wide" if i < QT else "probT")

@@ -44,7 +44,7 @@ def tile_attend_soft_draft_segb2q256n512t2048_kernel(
         qs = held.tile([P, B * NQ // 4], I32, name="qs", align_bytes=64)
         pos_pool = held.tile([P, T], F32, name="pos_pool")
         vs_pool = held.tile([P, T], F32, name="vs_pool")
-        qp = held.tile([P, TILES], F32, name="qp")
+        qp = held.tile([P, P], F32, name="qp")
         qbias = held.tile([P, TILES], F32, name="qbias")
         v_raw = [held.tile([P, T], F32, name=f"v_raw{f}") for f in range(2)]
         v_pool = [held.tile([P, T], BF16, name=f"v_pool{f}") for f in range(2)]
@@ -57,10 +57,10 @@ def tile_attend_soft_draft_segb2q256n512t2048_kernel(
         make_identity(nc, ident[:])
         nc.gpsimd.memset(ks_pool[:], 0)
         nc.gpsimd.memset(qs[:], 0)
+        nc.gpsimd.memset(qp[0 : P - TILES, :], 0.0)
         nc.vector.memset(warm[:, 0:1], 0.0)
         nc.vector.memset(pos_pool[0:LIVE, :], 0.0)
-        nc.vector.memset(vs_pool[0:LIVE, 0:SEG], 0.0)
-        nc.gpsimd.memset(vs_pool[0:LIVE, SEG:T], 0.0)
+        nc.vector.memset(vs_pool[0:LIVE, :], 0.0)
 
         def own(b):
             return slice(b * SEG, (b + 1) * SEG)
@@ -84,11 +84,10 @@ def tile_attend_soft_draft_segb2q256n512t2048_kernel(
         halves = [slice(0, SEG // 2), slice(SEG // 2, SEG)]
         nc.scalar.dma_start(pos_pool[LIVE:P, :], pos[0:1, :])
         nc.scalar.dma_start(vs_pool[LIVE:P, :], vs[0:1, :])
-        with nc.allow_non_contiguous_dma(reason="one place a query row"):
-            nc.sync.dma_start(qp[:], qpos.rearrange("b (h p) o -> p (b h o)", p=P))
         nc.sync.dma_start(offsets[:], offs)
-        for cols in halves:
-            load_v(0, cols)
+        load_v(0, halves[0])
+        nc.sync.dma_start(qp[P - TILES : P, :], qpos.rearrange("b (h p) o -> (b h) (p o)", p=P))
+        load_v(0, halves[1])
         load_v(1, own(0))
         load_v(0, own(1))
         load_ks(0)
@@ -244,11 +243,12 @@ def tile_attend_soft_draft_segb2q256n512t2048_kernel(
         pos_turned = turn_row(pos_pool, "pos", lambda row, j: row[:, j * P : (j + 1) * P])
         for cols in halves:
             cast_v(0, cols)
-        nc.scalar.mul(qbias[:], qp[:], -STRETCH)
         gather_v(0, 0)
         cast_v(1, own(0))
-        widen_pos(pos_turned)
         gather_v(0, 1)
+        nc.tensor.transpose(pos_turned[:, N - P : N], qp[:], ident[:])
+        nc.scalar.mul(qbias[:], pos_turned[:, N - TILES : N], -STRETCH)
+        widen_pos(pos_turned)
         nc.vector.tensor_copy(ks[:], ks_pool[:].bitcast(U8).indirect(offsets[:]))
         for b in range(B):
             gather_kw(b)

@@ -49,7 +49,6 @@ def tile_attend_soft_draft_segb2q256n512t2048_kernel(
         v_raw = [held.tile([P, T], F32, name=f"v_raw{f}") for f in range(2)]
         v_pool = [held.tile([P, T], BF16, name=f"v_pool{f}") for f in range(2)]
         ident = held.tile([P, P], F32, name="ident")
-        warm = held.tile([P, 2], F32, name="warm")
         negm = [held.tile([P, 1], F32, name=f"negm{i}") for i in range(TILES)]
         totals = held.tile([P, TILES], F32, name="totals")
         invs = held.tile([P, TILES], F32, name="invs")
@@ -58,7 +57,6 @@ def tile_attend_soft_draft_segb2q256n512t2048_kernel(
         nc.gpsimd.memset(ks_pool[:], 0)
         nc.gpsimd.memset(qs[:], 0)
         nc.gpsimd.memset(qp[0 : P - TILES, :], 0.0)
-        nc.vector.memset(warm[:, 0:1], 0.0)
         nc.vector.memset(pos_pool[0:LIVE, :], 0.0)
         nc.vector.memset(vs_pool[0:LIVE, :], 0.0)
 
@@ -101,8 +99,6 @@ def tile_attend_soft_draft_segb2q256n512t2048_kernel(
         load_kw(1)
         for g in range(1, 4):
             load_qs(g)
-
-        nc.scalar.activation(warm[:, 1:2], warm[:, 0:1], ACT.Exp)
 
         def listed(b):
             return offsets[:, b * COLS : (b + 1) * COLS]

@@ -46,8 +46,7 @@ def tile_attend_soft_draft_segb2q256n512t2048_kernel(
         vs_pool = held.tile([P, T], F32, name="vs_pool")
         qp = held.tile([P, P], F32, name="qp")
         qbias = held.tile([P, TILES], F32, name="qbias")
-        v_raw = [held.tile([P, T], F32, name=f"v_raw{f}") for f in range(2)]
-        v_pool = [held.tile([P, T], BF16, name=f"v_pool{f}") for f in range(2)]
+        v_pool = [held.tile([P, T], F32, name=f"v_pool{f}") for f in range(2)]
         ident = held.tile([P, P], F32, name="ident")
         negm = [held.tile([P, 1], F32, name=f"negm{i}") for i in range(TILES)]
         totals = held.tile([P, TILES], F32, name="totals")
@@ -67,8 +66,8 @@ def tile_attend_soft_draft_segb2q256n512t2048_kernel(
             words = k_words[0].rearrange("p n t -> p (n t)")
             nc.sync.dma_start(kw_pool[:, own(b)].bitcast(I32), words[:, PACK * b * SEG : PACK * (b + 1) * SEG].bitcast(I32))
 
-        def load_v(f, cols):
-            nc.sync.dma_start(v_raw[f][:, cols], vT[f * P : (f + 1) * P, cols])
+        def load_v(f):
+            nc.sync.dma_start(v_pool[f][:], vT[f * P : (f + 1) * P, :])
 
         def load_ks(g):
             nc.sync.dma_start(ks_pool[32 * g : 32 * g + 4, :], k_scales[0, 4 * g : 4 * g + 4, :].bitcast(I32))
@@ -79,26 +78,23 @@ def tile_attend_soft_draft_segb2q256n512t2048_kernel(
                 q_scales[:, 0, 4 * g : 4 * g + 4, :].rearrange("b f q -> f b q").bitcast(I32),
             )
 
-        halves = [slice(0, SEG // 2), slice(SEG // 2, SEG)]
         nc.scalar.dma_start(pos_pool[LIVE:P, :], pos[0:1, :])
         nc.scalar.dma_start(vs_pool[LIVE:P, :], vs[0:1, :])
         nc.sync.dma_start(offsets[:], offs)
-        load_v(0, halves[0])
         nc.sync.dma_start(qp[P - TILES : P, :], qpos.rearrange("b (h p) o -> (b h) (p o)", p=P))
-        load_v(0, halves[1])
-        load_v(1, own(0))
-        load_v(0, own(1))
+        load_v(0)
         load_ks(0)
         load_ks(1)
-        load_qs(0)
-        load_kw(0)
-        load_v(1, own(1))
-        nc.sync.dma_start(qw[:].bitcast(I32), q_words[:, 0].rearrange("b p q t -> p b (q t)").bitcast(I32))
         load_ks(2)
         load_ks(3)
+        load_kw(0)
+        load_v(1)
+        load_qs(0)
+        load_qs(1)
         load_kw(1)
-        for g in range(1, 4):
-            load_qs(g)
+        nc.sync.dma_start(qw[:].bitcast(I32), q_words[:, 0].rearrange("b p q t -> p b (q t)").bitcast(I32))
+        load_qs(2)
+        load_qs(3)
 
         def listed(b):
             return offsets[:, b * COLS : (b + 1) * COLS]
@@ -114,9 +110,12 @@ def tile_attend_soft_draft_segb2q256n512t2048_kernel(
         vsc = held.tile([P, B * DV], U8, name="vsc", align_bytes=64)
         w_pair = held.tile([P, QT, P, PACK], BF16, name="w_pair", align_bytes=64)
 
-        def turn_row(pool, name, piece):
+        def turn_row(pool, name, piece, on_scalar):
             row = held.tile([P, B * N], F32, name=name + "_row")
-            nc.vector.tensor_copy(row[:], pool[:].indirect(offsets[:]))
+            if on_scalar:
+                nc.scalar.activation(row[:], pool[:].indirect(offsets[:]), ACT.Copy)
+            else:
+                nc.vector.tensor_copy(row[:], pool[:].indirect(offsets[:]))
             turned = psum.tile([P, N], F32, name="turned", tag="turned")
             for j in reversed(range(CHUNKS)):
                 nc.tensor.transpose(turned[:, 2 * j : 2 * j + P], piece(row, j), ident[:])
@@ -141,21 +140,16 @@ def tile_attend_soft_draft_segb2q256n512t2048_kernel(
             kw[b] = held.tile([P, N], U32, name=f"kw{b}", align_bytes=64)
             nc.vector.tensor_copy(kw[b][:], kw_pool[:, window(b)].indirect(listed(b)))
 
-        def cast_v(f, cols):
-            nc.scalar.activation(v_pool[f][:, cols], v_raw[f][:, cols], ACT.Copy)
-
         def gather_v(b, f):
-            v_listed[b, f] = held.tile([P, 2, P, 2], BF16, name=f"v_listed{b}{f}")
-            nc.scalar.activation(
-                v_listed[b, f][:].rearrange("e u s j -> e s u j"), v_pool[f][:, window(b)].indirect(listed(b)), ACT.Copy
-            )
+            v_listed[b, f] = held.tile([P, N], BF16, name=f"v_listed{b}{f}")
+            nc.scalar.activation(v_listed[b, f][:], v_pool[f][:].indirect(listed(b)), ACT.Copy)
 
         def turn_v(b, tag):
             turned = psum.tile([P, 2, 2, P], F32, name="turned_v", tag=tag)
             for f in range(2):
-                pairs = v_listed[b, f][:].rearrange("e u s j -> e (u s j)").bitcast(F32)
+                pairs = v_listed[b, f][:].bitcast(F32)
                 for u in range(2):
-                    nc.tensor.transpose(turned[:, f, u, :], pairs[:, u * P : (u + 1) * P], ident[:])
+                    nc.tensor.transpose(turned[:, f, u, :], pairs[:, u : 2 * P : 2], ident[:])
             nc.scalar.copy(
                 vt[:, b].rearrange("s e t -> s (e t)").bitcast(F32).rearrange("s (f e u) -> s f e u", f=2, u=2),
                 turned[:].rearrange("s f u e -> s f e u"),
@@ -236,20 +230,20 @@ def tile_attend_soft_draft_segb2q256n512t2048_kernel(
                 nc.scalar.activation(y[:], acc[:, 0:DV], ACT.Copy, scale=invs[:, i : i + 1])
             nc.sync.dma_start(out[b, h * P : (h + 1) * P, :], y[:])
 
-        pos_turned = turn_row(pos_pool, "pos", lambda row, j: row[:, j * P : (j + 1) * P])
-        for cols in halves:
-            cast_v(0, cols)
+        pos_turned = turn_row(pos_pool, "pos", lambda row, j: row[:, j * P : (j + 1) * P], True)
+        vs_turned = turn_row(
+            vs_pool, "vs", lambda row, j: row[:, (j // PACK) * N + j % PACK : (j // PACK + 1) * N : PACK], False
+        )
         gather_v(0, 0)
-        cast_v(1, own(0))
-        gather_v(0, 1)
         nc.tensor.transpose(pos_turned[:, N - P : N], qp[:], ident[:])
         nc.scalar.mul(qbias[:], pos_turned[:, N - TILES : N], -STRETCH)
         widen_pos(pos_turned)
+        gather_v(1, 0)
+        vs_col = live_columns(vs_turned, "vs")
         nc.vector.tensor_copy(ks[:], ks_pool[:].bitcast(U8).indirect(offsets[:]))
         for b in range(B):
             gather_kw(b)
-        nc.vector.tensor_copy(v_pool[1][:, own(1)], v_raw[1][:, own(1)])
-        cast_v(0, own(1))
+        gather_v(0, 1)
         for i in range(TILES):
             make_penalty(i)
 
@@ -257,8 +251,7 @@ def tile_attend_soft_draft_segb2q256n512t2048_kernel(
             scores(i)
         for i in range(QT):
             apply_mask(i)
-        for f in range(2):
-            gather_v(1, f)
+        gather_v(1, 1)
         for i in range(QT, TILES):
             scores(i)
         for i in range(QT):
@@ -267,8 +260,6 @@ def tile_attend_soft_draft_segb2q256n512t2048_kernel(
         turn_v(0, "turned")
         turn_p(0, "probT")
         weigh(2)
-        vs_turned = turn_row(vs_pool, "vs", lambda row, j: row[:, (j // PACK) * N + j % PACK : (j // PACK + 1) * N : PACK])
-        vs_col = live_columns(vs_turned, "vs")
         weigh(3)
         turn_v(1, "score")
         turn_p(1, "probT")

@@ -35,6 +35,7 @@ def tile_attend_soft_draft_segb2q256n512t2048_kernel(
     nc = tc.nc
     with ExitStack() as ctx:
         held = ctx.enter_context(tc.tile_pool(name="held", bufs=1))
+        reused = ctx.enter_context(tc.tile_pool(name="reused", bufs=1))
         psum = ctx.enter_context(tc.psum_pool(name="psum", bufs=2))
 
         offsets = held.tile([P, B * COLS], U16, name="offsets")
@@ -46,25 +47,20 @@ def tile_attend_soft_draft_segb2q256n512t2048_kernel(
         vs_pool = held.tile([P, T], F32, name="vs_pool")
         qp = held.tile([P, P], F32, name="qp")
         qbias = held.tile([P, TILES], F32, name="qbias")
-        v_pool = [held.tile([P, T], F32, name=f"v_pool{f}") for f in range(2)]
+        v_pool = [reused.tile([P, T], F32, name=f"v_pool{f}", offset=4 * T * f) for f in range(2)]
         ident = held.tile([P, P], F32, name="ident")
         negm = [held.tile([P, 1], F32, name=f"negm{i}") for i in range(TILES)]
         totals = held.tile([P, TILES], F32, name="totals")
         invs = held.tile([P, TILES], F32, name="invs")
 
-        make_identity(nc, ident[:])
         nc.gpsimd.memset(ks_pool[:], 0)
         nc.gpsimd.memset(qs[:], 0)
-        nc.gpsimd.memset(qp[0 : P - TILES, :], 0.0)
+        make_identity(nc, ident[:])
+        zero = held.tile([P, 1], F32, name="zero")
+        nc.vector.memset(zero[:], 0.0)
+        nc.scalar.activation(qp[0 : P - TILES, :], zero[0 : P - TILES, :].to_broadcast([P - TILES, P]), ACT.Copy)
         nc.vector.memset(pos_pool[0:LIVE, :], 0.0)
         nc.vector.memset(vs_pool[0:LIVE, :], 0.0)
-
-        def own(b):
-            return slice(b * SEG, (b + 1) * SEG)
-
-        def load_kw(b):
-            words = k_words[0].rearrange("p n t -> p (n t)")
-            nc.sync.dma_start(kw_pool[:, own(b)].bitcast(I32), words[:, PACK * b * SEG : PACK * (b + 1) * SEG].bitcast(I32))
 
         def load_v(f):
             nc.sync.dma_start(v_pool[f][:], vT[f * P : (f + 1) * P, :])
@@ -79,22 +75,17 @@ def tile_attend_soft_draft_segb2q256n512t2048_kernel(
             )
 
         nc.scalar.dma_start(pos_pool[LIVE:P, :], pos[0:1, :])
-        nc.scalar.dma_start(vs_pool[LIVE:P, :], vs[0:1, :])
         nc.sync.dma_start(offsets[:], offs)
-        nc.sync.dma_start(qp[P - TILES : P, :], qpos.rearrange("b (h p) o -> (b h) (p o)", p=P))
-        load_v(0)
-        load_ks(0)
-        load_ks(1)
-        load_ks(2)
-        load_ks(3)
-        load_kw(0)
-        load_v(1)
-        load_qs(0)
-        load_qs(1)
-        load_kw(1)
         nc.sync.dma_start(qw[:].bitcast(I32), q_words[:, 0].rearrange("b p q t -> p b (q t)").bitcast(I32))
-        load_qs(2)
-        load_qs(3)
+        for g in range(4):
+            load_ks(g)
+        nc.sync.dma_start(kw_pool[:].bitcast(I32), k_words[0].rearrange("p n t -> p (n t)").bitcast(I32))
+        nc.sync.dma_start(qp[P - TILES : P, :], qpos.rearrange("b (h p) o -> (b h) (p o)", p=P))
+        nc.sync.dma_start(vs_pool[LIVE:P, :], vs[0:1, :])
+        for g in range(4):
+            load_qs(g)
+        load_v(0)
+        load_v(1)
 
         def listed(b):
             return offsets[:, b * COLS : (b + 1) * COLS]
@@ -108,33 +99,31 @@ def tile_attend_soft_draft_segb2q256n512t2048_kernel(
         vt = held.tile([P, B, DV, PACK], BF16, name="vt", align_bytes=64)
         vq = held.tile([P, B * DV], U32, name="vq", align_bytes=64)
         vsc = held.tile([P, B * DV], U8, name="vsc", align_bytes=64)
+        vs_col = [held.tile([P, PACK], F32, name=f"vs_col{b}") for b in range(B)]
         w_pair = held.tile([P, QT, P, PACK], BF16, name="w_pair", align_bytes=64)
 
-        def turn_row(pool, name, piece, on_scalar):
-            row = held.tile([P, B * N], F32, name=name + "_row")
-            if on_scalar:
-                nc.scalar.activation(row[:], pool[:].indirect(offsets[:]), ACT.Copy)
-            else:
-                nc.vector.tensor_copy(row[:], pool[:].indirect(offsets[:]))
+        def turn_pos(b):
+            row = held.tile([P, N], F32, name=f"pos_row{b}")
+            nc.scalar.activation(row[:], pos_pool[:, window(b)].indirect(listed(b)), ACT.Copy)
             turned = psum.tile([P, N], F32, name="turned", tag="turned")
-            for j in reversed(range(CHUNKS)):
-                nc.tensor.transpose(turned[:, 2 * j : 2 * j + P], piece(row, j), ident[:])
+            for j in reversed(range(PACK)):
+                nc.tensor.transpose(turned[:, 2 * j : 2 * j + P], row[:, j * P : (j + 1) * P], ident[:])
             return turned
 
-        def live_columns(turned, name):
-            col = held.tile([P, CHUNKS], F32, name=name + "_col")
-            nc.scalar.copy(col[:], turned[:, LIVE : LIVE + 2 * CHUNKS : 2])
-            return col
+        def widen_pos(b, turned):
+            col = held.tile([P, PACK], F32, name=f"pos_col{b}")
+            nc.scalar.copy(col[:], turned[:, LIVE : LIVE + 2 * PACK : 2])
+            pos_wide[b] = psum.tile([P, N], F32, name="pos_wide", tag="pos_wide")
+            for c in range(N // P):
+                nc.tensor.transpose(
+                    pos_wide[b][:, c * P : (c + 1) * P], col[:, c : c + 1].to_broadcast([P, P]), ident[:]
+                )
 
-        def widen_pos(turned):
-            col = live_columns(turned, "pos")
+        def deal_vs():
+            row = held.tile([P, B * N], F32, name="vs_row")
+            nc.vector.tensor_copy(row[:], vs_pool[:].indirect(offsets[:]))
             for b in range(B):
-                pos_wide[b] = psum.tile([P, N], F32, name="pos_wide", tag="pos_wide")
-                for c in range(N // P):
-                    j = b * (N // P) + c
-                    nc.tensor.transpose(
-                        pos_wide[b][:, c * P : (c + 1) * P], col[:, j : j + 1].to_broadcast([P, P]), ident[:]
-                    )
+                nc.sync.dma_start(vs_col[b][:], row[LIVE:P, b * N : (b + 1) * N])
 
         def gather_kw(b):
             kw[b] = held.tile([P, N], U32, name=f"kw{b}", align_bytes=64)
@@ -178,7 +167,7 @@ def tile_attend_soft_draft_segb2q256n512t2048_kernel(
 
         def weigh(i):
             nc.vector.tensor_reduce(negm[i][:], negs[i][:], AX.X, ALU.min)
-            prob[i] = held.tile([P, PACK, P], F32, name=f"prob{i}")
+            prob[i] = reused.tile([P, PACK, P], F32, name=f"prob{i}", offset=4 * T + 4 * N * i)
             nc.scalar.activation(
                 prob[i][:].rearrange("q t s -> q s t"),
                 negs[i][:].rearrange("q (s t) -> q s t", t=PACK),
@@ -193,13 +182,13 @@ def tile_attend_soft_draft_segb2q256n512t2048_kernel(
             for t in range(PACK):
                 nc.tensor.transpose(probT[i][:, t, :], prob[i][:, t, :], ident[:])
 
-        def scale_w(i, vs_col):
+        def scale_w(i):
             b = i // QT
             wT[i] = w_pair[:, i] if b == 0 else held.tile([P, P, PACK], BF16, name=f"wT{i}", align_bytes=64)
             nc.vector.tensor_tensor(
                 wT[i][:],
                 probT[i][:].rearrange("s t q -> s q t"),
-                vs_col[:, PACK * b : PACK * (b + 1)].unsqueeze(1).to_broadcast([P, P, PACK]),
+                vs_col[b][:].unsqueeze(1).to_broadcast([P, P, PACK]),
                 ALU.mult,
             )
 
@@ -230,49 +219,46 @@ def tile_attend_soft_draft_segb2q256n512t2048_kernel(
                 nc.scalar.activation(y[:], acc[:, 0:DV], ACT.Copy, scale=invs[:, i : i + 1])
             nc.sync.dma_start(out[b, h * P : (h + 1) * P, :], y[:])
 
-        pos_turned = turn_row(pos_pool, "pos", lambda row, j: row[:, j * P : (j + 1) * P], True)
-        vs_turned = turn_row(
-            vs_pool, "vs", lambda row, j: row[:, (j // PACK) * N + j % PACK : (j // PACK + 1) * N : PACK], False
-        )
-        gather_v(0, 0)
-        nc.tensor.transpose(pos_turned[:, N - P : N], qp[:], ident[:])
-        nc.scalar.mul(qbias[:], pos_turned[:, N - TILES : N], -STRETCH)
-        widen_pos(pos_turned)
-        gather_v(1, 0)
-        vs_col = live_columns(vs_turned, "vs")
+        pos_turned = [turn_pos(b) for b in range(B)]
+        widen_pos(0, pos_turned[0])
+        nc.tensor.transpose(pos_turned[1][:, N - P : N], qp[:], ident[:])
+        nc.scalar.mul(qbias[:], pos_turned[1][:, N - TILES : N], -STRETCH)
+        widen_pos(1, pos_turned[1])
         nc.vector.tensor_copy(ks[:], ks_pool[:].bitcast(U8).indirect(offsets[:]))
         for b in range(B):
             gather_kw(b)
-        gather_v(0, 1)
+        deal_vs()
         for i in range(TILES):
             make_penalty(i)
+        for f in range(2):
+            for b in range(B):
+                gather_v(b, f)
 
         for i in range(QT):
             scores(i)
         for i in range(QT):
             apply_mask(i)
-        gather_v(1, 1)
         for i in range(QT, TILES):
             scores(i)
         for i in range(QT):
             weigh(i)
             apply_mask(i + QT)
         turn_v(0, "turned")
+        turn_v(1, "turned")
         turn_p(0, "probT")
+        turn_p(1, "probT")
         weigh(2)
         weigh(3)
-        turn_v(1, "score")
-        turn_p(1, "probT")
-        for i in range(QT, TILES):
-            turn_p(i, "turned")
+        turn_p(2, "score")
+        turn_p(3, "score")
 
-        scale_w(0, vs_col)
+        scale_w(0)
         nc.vector.quantize_mx(vq[:].bitcast(FP8X4), vsc[:], vt[:].rearrange("s b e t -> s (b e t)"))
-        scale_w(1, vs_col)
+        scale_w(1)
         nc.vector.reciprocal(invs[:], totals[:])
-        scale_w(2, vs_col)
+        scale_w(2)
         quantize_w([0, 1], w_pair[:].rearrange("s i q t -> s (i q t)"))
-        scale_w(3, vs_col)
+        scale_w(3)
         for i in range(QT, TILES):
             quantize_w([i], wT[i][:].rearrange("s q t -> s (q t)"))
         for i in range(TILES):

@@ -27,6 +27,8 @@ CHUNKS = B * N // P
 LIVE = P - 1
 STRETCH = 2.0**80
 PENALTY = 2.0**50
+V_AT = 6 * 1024
+QP_AT = 12
 
 
 def tile_attend_soft_draft_segb2q256n512t2048_kernel(
@@ -46,8 +48,7 @@ def tile_attend_soft_draft_segb2q256n512t2048_kernel(
         pos_pool = held.tile([P, T], F32, name="pos_pool")
         vs_pool = held.tile([P, T], F32, name="vs_pool")
         qp = held.tile([P, P], F32, name="qp")
-        qbias = held.tile([P, TILES], F32, name="qbias")
-        v_pool = [reused.tile([P, T], F32, name=f"v_pool{f}", offset=4 * T * f) for f in range(2)]
+        v_pool = [reused.tile([P, T], F32, name=f"v_pool{f}", offset=V_AT + 4 * T * f) for f in range(2)]
         ident = held.tile([P, P], F32, name="ident")
         negm = [held.tile([P, 1], F32, name=f"negm{i}") for i in range(TILES)]
         totals = held.tile([P, TILES], F32, name="totals")
@@ -94,11 +95,9 @@ def tile_attend_soft_draft_segb2q256n512t2048_kernel(
             return slice(0, (b + 1) * SEG)
 
         kw, pos_wide, v_listed = {}, {}, {}
-        score, penalty, negs, prob, probT, wT, wq, wsc = {}, {}, {}, {}, {}, {}, {}, {}
+        score, negs, prob, probT, wT, wq, wsc = {}, {}, {}, {}, {}, {}, {}
         ks = held.tile([P, B * N], U8, name="ks", align_bytes=64)
-        vt = held.tile([P, B, DV, PACK], BF16, name="vt", align_bytes=64)
-        vq = held.tile([P, B * DV], U32, name="vq", align_bytes=64)
-        vsc = held.tile([P, B * DV], U8, name="vsc", align_bytes=64)
+        vt, vq, vsc = {}, {}, {}
         vs_col = [held.tile([P, PACK], F32, name=f"vs_col{b}") for b in range(B)]
         w_pair = held.tile([P, QT, P, PACK], BF16, name="w_pair", align_bytes=64)
 
@@ -106,21 +105,21 @@ def tile_attend_soft_draft_segb2q256n512t2048_kernel(
             row = held.tile([P, N], F32, name=f"pos_row{b}")
             nc.scalar.activation(row[:], pos_pool[:, window(b)].indirect(listed(b)), ACT.Copy)
             turned = psum.tile([P, N], F32, name="turned", tag="turned")
+            if b == 0:
+                nc.tensor.transpose(turned[:, QP_AT : QP_AT + P], qp[:], ident[:])
             for j in reversed(range(PACK)):
                 nc.tensor.transpose(turned[:, 2 * j : 2 * j + P], row[:, j * P : (j + 1) * P], ident[:])
             return turned
 
-        def widen_pos(b, turned):
-            col = held.tile([P, PACK], F32, name=f"pos_col{b}")
-            nc.scalar.copy(col[:], turned[:, LIVE : LIVE + 2 * PACK : 2])
+        def widen_pos(b, col):
             pos_wide[b] = psum.tile([P, N], F32, name="pos_wide", tag="pos_wide")
             for c in range(N // P):
                 nc.tensor.transpose(
-                    pos_wide[b][:, c * P : (c + 1) * P], col[:, c : c + 1].to_broadcast([P, P]), ident[:]
+                    pos_wide[b][:, c * P : (c + 1) * P], col[:, 2 * c : 2 * c + 1].to_broadcast([P, P]), ident[:]
                 )
 
         def deal_vs():
-            row = held.tile([P, B * N], F32, name="vs_row")
+            row = reused.tile([P, B * N], F32, name="vs_row", offset=V_AT + 4 * T - 4 * B * N)
             nc.vector.tensor_copy(row[:], vs_pool[:].indirect(offsets[:]))
             for b in range(B):
                 nc.sync.dma_start(vs_col[b][:], row[LIVE:P, b * N : (b + 1) * N])
@@ -131,7 +130,10 @@ def tile_attend_soft_draft_segb2q256n512t2048_kernel(
 
         def gather_v(b, f):
             v_listed[b, f] = held.tile([P, N], BF16, name=f"v_listed{b}{f}")
-            nc.scalar.activation(v_listed[b, f][:], v_pool[f][:].indirect(listed(b)), ACT.Copy)
+            if (b, f) == (1, 0):
+                nc.vector.tensor_copy(v_listed[b, f][:], v_pool[f][:].indirect(listed(b)))
+            else:
+                nc.scalar.activation(v_listed[b, f][:], v_pool[f][:].indirect(listed(b)), ACT.Copy)
 
         def turn_v(b, tag):
             turned = psum.tile([P, 2, 2, P], F32, name="turned_v", tag=tag)
@@ -139,10 +141,19 @@ def tile_attend_soft_draft_segb2q256n512t2048_kernel(
                 pairs = v_listed[b, f][:].bitcast(F32)
                 for u in range(2):
                     nc.tensor.transpose(turned[:, f, u, :], pairs[:, u : 2 * P : 2], ident[:])
+            return turned
+
+        def copy_v(b, turned):
+            vt[b] = reused.tile([P, DV, PACK], BF16, name=f"vt{b}", offset=V_AT + 8 * T + 4 * N * (b + 1), align_bytes=64)
             nc.scalar.copy(
-                vt[:, b].rearrange("s e t -> s (e t)").bitcast(F32).rearrange("s (f e u) -> s f e u", f=2, u=2),
+                vt[b][:].rearrange("s e t -> s (e t)").bitcast(F32).rearrange("s (f e u) -> s f e u", f=2, u=2),
                 turned[:].rearrange("s f u e -> s f e u"),
             )
+
+        def quantize_v(b):
+            vq[b] = held.tile([P, DV], U32, name=f"vq{b}", align_bytes=64)
+            vsc[b] = held.tile([P, DV], U8, name=f"vsc{b}", align_bytes=64)
+            nc.vector.quantize_mx(vq[b][:].bitcast(FP8X4), vsc[b][:], vt[b][:].rearrange("s e t -> s (e t)"))
 
         def scores(i):
             b, h = divmod(i, QT)
@@ -158,23 +169,25 @@ def tile_attend_soft_draft_segb2q256n512t2048_kernel(
             )
 
         def make_penalty(i):
-            penalty[i] = held.tile([P, N], F32, name=f"penalty{i}")
-            nc.scalar.activation(penalty[i][:], pos_wide[i // QT][:], ACT.Relu, bias=qbias[:, i : i + 1], scale=STRETCH)
+            nc.scalar.activation(
+                penalty[:, i],
+                pos_wide[i // QT][:].rearrange("q (s t) -> q t s", t=PACK),
+                ACT.Relu,
+                bias=qbias[:, i : i + 1],
+                scale=-1.0,
+            )
 
         def apply_mask(i):
-            negs[i] = held.tile([P, N], F32, name=f"negs{i}")
-            nc.vector.scalar_tensor_tensor(negs[i][:], penalty[i][:], PENALTY, score[i][:], ALU.min, ALU.subtract)
+            negs[i] = reused.tile([P, PACK, P], F32, name=f"negs{i}", offset=V_AT + 8 * T + 4 * N * i)
+            nc.vector.scalar_tensor_tensor(
+                negs[i][:], penalty[:, i], PENALTY, score[i][:].rearrange("q (s t) -> q t s", t=PACK), ALU.min, ALU.subtract
+            )
 
         def weigh(i):
-            nc.vector.tensor_reduce(negm[i][:], negs[i][:], AX.X, ALU.min)
-            prob[i] = reused.tile([P, PACK, P], F32, name=f"prob{i}", offset=4 * T + 4 * N * i)
+            nc.vector.tensor_reduce(negm[i][:], negs[i][:].rearrange("q t s -> q (t s)"), AX.X, ALU.min)
+            prob[i] = reused.tile([P, PACK, P], F32, name=f"prob{i}", offset=V_AT + 4 * T + 4 * N * i)
             nc.scalar.activation(
-                prob[i][:].rearrange("q t s -> q s t"),
-                negs[i][:].rearrange("q (s t) -> q s t", t=PACK),
-                ACT.Exp,
-                bias=negm[i][:],
-                scale=-1.0,
-                accum_out=totals[:, i : i + 1],
+                prob[i][:], negs[i][:], ACT.Exp, bias=negm[i][:], scale=-1.0, accum_out=totals[:, i : i + 1]
             )
 
         def turn_p(i, tag):
@@ -207,8 +220,8 @@ def tile_attend_soft_draft_segb2q256n512t2048_kernel(
                 acc[:, 0:DV],
                 lhsT=wq[i].bitcast(FP8X4),
                 lhsT_scale=wsc[i],
-                rhs=vq[:, b * DV : (b + 1) * DV].bitcast(FP8X4),
-                rhs_scale=vsc[:, b * DV : (b + 1) * DV],
+                rhs=vq[b][:].bitcast(FP8X4),
+                rhs_scale=vsc[b][:],
                 start=True,
                 stop=True,
             )
@@ -220,19 +233,24 @@ def tile_attend_soft_draft_segb2q256n512t2048_kernel(
             nc.sync.dma_start(out[b, h * P : (h + 1) * P, :], y[:])
 
         pos_turned = [turn_pos(b) for b in range(B)]
-        widen_pos(0, pos_turned[0])
-        nc.tensor.transpose(pos_turned[1][:, N - P : N], qp[:], ident[:])
-        nc.scalar.mul(qbias[:], pos_turned[1][:, N - TILES : N], -STRETCH)
-        widen_pos(1, pos_turned[1])
+        first = held.tile([P, QP_AT + 1], F32, name="first")
+        nc.scalar.mul(first[:], pos_turned[0][:, LIVE : QP_AT + P], -STRETCH)
+        qbias = first[:, QP_AT + 1 - TILES :]
+        widen_pos(0, first)
         nc.vector.tensor_copy(ks[:], ks_pool[:].bitcast(U8).indirect(offsets[:]))
         for b in range(B):
             gather_kw(b)
+        for b in range(B):
+            gather_v(b, 0)
+        second = reused.tile([P, 2 * PACK], F32, name="second", offset=4 * TILES * N)
+        nc.scalar.mul(second[:, 0 : 2 * PACK - 1], pos_turned[1][:, LIVE : LIVE + 2 * PACK - 1], -STRETCH)
+        widen_pos(1, second)
         deal_vs()
+        penalty = reused.tile([P, TILES, PACK, P], F32, name="penalty", offset=0)
         for i in range(TILES):
             make_penalty(i)
-        for f in range(2):
-            for b in range(B):
-                gather_v(b, f)
+        for b in range(B):
+            gather_v(b, 1)
 
         for i in range(QT):
             scores(i)
@@ -243,23 +261,25 @@ def tile_attend_soft_draft_segb2q256n512t2048_kernel(
         for i in range(QT):
             weigh(i)
             apply_mask(i + QT)
-        turn_v(0, "turned")
-        turn_v(1, "turned")
+        v_turned = [turn_v(b, "turned") for b in range(B)]
         turn_p(0, "probT")
         turn_p(1, "probT")
         weigh(2)
         weigh(3)
+        for b in range(B):
+            copy_v(b, v_turned[b])
         turn_p(2, "score")
         turn_p(3, "score")
 
         scale_w(0)
-        nc.vector.quantize_mx(vq[:].bitcast(FP8X4), vsc[:], vt[:].rearrange("s b e t -> s (b e t)"))
         scale_w(1)
-        nc.vector.reciprocal(invs[:], totals[:])
         scale_w(2)
         quantize_w([0, 1], w_pair[:].rearrange("s i q t -> s (i q t)"))
+        nc.vector.reciprocal(invs[:], totals[:])
         scale_w(3)
+        quantize_v(0)
         for i in range(QT, TILES):
             quantize_w([i], wT[i][:].rearrange("s q t -> s (q t)"))
+        quantize_v(1)
         for i in range(TILES):
             finish(i, "pos_wide" if i < QT else "probT")

@@ -28,7 +28,7 @@ LIVE = P - 1
 STRETCH = 2.0**80
 PENALTY = 2.0**50
 V_AT = 6 * 1024
-QP_AT = 12
+QP_AT = 20
 
 
 def tile_attend_soft_draft_segb2q256n512t2048_kernel(
@@ -42,13 +42,17 @@ def tile_attend_soft_draft_segb2q256n512t2048_kernel(
 
         offsets = held.tile([P, B * COLS], U16, name="offsets")
         kw_pool = held.tile([P, T], U32, name="kw_pool")
-        ks_pool = held.tile([P, T // 4], I32, name="ks_pool")
+        ks_pool = reused.tile([P, T // 4], I32, name="ks_pool", offset=0)
         qw = held.tile([P, B, NQ], U32, name="qw", align_bytes=64)
         qs = held.tile([P, B * NQ // 4], I32, name="qs", align_bytes=64)
         pos_pool = held.tile([P, T], F32, name="pos_pool")
         vs_pool = held.tile([P, T], F32, name="vs_pool")
         qp = held.tile([P, P], F32, name="qp")
-        v_pool = [reused.tile([P, T], F32, name=f"v_pool{f}", offset=V_AT + 4 * T * f) for f in range(2)]
+        v_first = reused.tile([P, T], F32, name="v_first", offset=V_AT)
+        v_second = [
+            reused.tile([P, SEG], F32, name="v_second0", offset=V_AT + 4 * T),
+            reused.tile([P, T], F32, name="v_second1", offset=V_AT + 4 * T + 4 * SEG),
+        ]
         ident = held.tile([P, P], F32, name="ident")
         negm = [held.tile([P, 1], F32, name=f"negm{i}") for i in range(TILES)]
         totals = held.tile([P, TILES], F32, name="totals")
@@ -56,15 +60,12 @@ def tile_attend_soft_draft_segb2q256n512t2048_kernel(
 
         nc.gpsimd.memset(ks_pool[:], 0)
         nc.gpsimd.memset(qs[:], 0)
-        make_identity(nc, ident[:])
+        nc.gpsimd.memset(qp[0 : P - TILES, :], 0.0)
         zero = held.tile([P, 1], F32, name="zero")
         nc.vector.memset(zero[:], 0.0)
-        nc.scalar.activation(qp[0 : P - TILES, :], zero[0 : P - TILES, :].to_broadcast([P - TILES, P]), ACT.Copy)
         nc.vector.memset(pos_pool[0:LIVE, :], 0.0)
         nc.vector.memset(vs_pool[0:LIVE, :], 0.0)
-
-        def load_v(f):
-            nc.sync.dma_start(v_pool[f][:], vT[f * P : (f + 1) * P, :])
+        nc.vector.memset(v_second[1][:, 0:SEG], 0.0)
 
         def load_ks(g):
             nc.sync.dma_start(ks_pool[32 * g : 32 * g + 4, :], k_scales[0, 4 * g : 4 * g + 4, :].bitcast(I32))
@@ -76,17 +77,21 @@ def tile_attend_soft_draft_segb2q256n512t2048_kernel(
             )
 
         nc.scalar.dma_start(pos_pool[LIVE:P, :], pos[0:1, :])
+        nc.scalar.activation(ident[:], zero[:].to_broadcast([P, P]), ACT.Copy)
+        make_identity(nc, ident[:], nomemset=True)
         nc.sync.dma_start(offsets[:], offs)
-        nc.sync.dma_start(qw[:].bitcast(I32), q_words[:, 0].rearrange("b p q t -> p b (q t)").bitcast(I32))
-        for g in range(4):
-            load_ks(g)
-        nc.sync.dma_start(kw_pool[:].bitcast(I32), k_words[0].rearrange("p n t -> p (n t)").bitcast(I32))
-        nc.sync.dma_start(qp[P - TILES : P, :], qpos.rearrange("b (h p) o -> (b h) (p o)", p=P))
         nc.sync.dma_start(vs_pool[LIVE:P, :], vs[0:1, :])
         for g in range(4):
+            load_ks(g)
+        nc.sync.dma_start(v_first[:], vT[0:P, :])
+        nc.sync.dma_start(qp[P - TILES : P, :], qpos.rearrange("b (h p) o -> (b h) (p o)", p=P))
+        nc.sync.dma_start(kw_pool[:].bitcast(I32), k_words[0].rearrange("p n t -> p (n t)").bitcast(I32))
+        nc.sync.dma_start(qw[:].bitcast(I32), q_words[:, 0].rearrange("b p q t -> p b (q t)").bitcast(I32))
+        for g in range(4):
             load_qs(g)
-        load_v(0)
-        load_v(1)
+        for b in range(B):
+            cols = slice(b * SEG, (b + 1) * SEG)
+            nc.sync.dma_start(v_second[b][:, cols], vT[P : 2 * P, cols])
 
         def listed(b):
             return offsets[:, b * COLS : (b + 1) * COLS]
@@ -104,22 +109,21 @@ def tile_attend_soft_draft_segb2q256n512t2048_kernel(
         def turn_pos(b):
             row = held.tile([P, N], F32, name=f"pos_row{b}")
             nc.scalar.activation(row[:], pos_pool[:, window(b)].indirect(listed(b)), ACT.Copy)
-            turned = psum.tile([P, N], F32, name="turned", tag="turned")
-            if b == 0:
-                nc.tensor.transpose(turned[:, QP_AT : QP_AT + P], qp[:], ident[:])
-            for j in reversed(range(PACK)):
-                nc.tensor.transpose(turned[:, 2 * j : 2 * j + P], row[:, j * P : (j + 1) * P], ident[:])
-            return turned
+            for c in range(N // P):
+                at = LIVE + place(b, c) - (P - 1)
+                nc.tensor.transpose(pos_turned[:, at : at + P], row[:, c * P : (c + 1) * P], ident[:])
 
-        def widen_pos(b, col):
+        def place(b, c):
+            return 2 * (CHUNKS - 1 - b * (N // P) - c)
+
+        def widen_pos(b):
             pos_wide[b] = psum.tile([P, N], F32, name="pos_wide", tag="pos_wide")
             for c in range(N // P):
-                nc.tensor.transpose(
-                    pos_wide[b][:, c * P : (c + 1) * P], col[:, 2 * c : 2 * c + 1].to_broadcast([P, P]), ident[:]
-                )
+                column = places[:, place(b, c) : place(b, c) + 1]
+                nc.tensor.transpose(pos_wide[b][:, c * P : (c + 1) * P], column.to_broadcast([P, P]), ident[:])
 
         def deal_vs():
-            row = reused.tile([P, B * N], F32, name="vs_row", offset=V_AT + 4 * T - 4 * B * N)
+            row = held.tile([P, B * N], F32, name="vs_row")
             nc.vector.tensor_copy(row[:], vs_pool[:].indirect(offsets[:]))
             for b in range(B):
                 nc.sync.dma_start(vs_col[b][:], row[LIVE:P, b * N : (b + 1) * N])
@@ -130,10 +134,7 @@ def tile_attend_soft_draft_segb2q256n512t2048_kernel(
 
         def gather_v(b, f):
             v_listed[b, f] = held.tile([P, N], BF16, name=f"v_listed{b}{f}")
-            if (b, f) == (1, 0):
-                nc.vector.tensor_copy(v_listed[b, f][:], v_pool[f][:].indirect(listed(b)))
-            else:
-                nc.scalar.activation(v_listed[b, f][:], v_pool[f][:].indirect(listed(b)), ACT.Copy)
+            nc.scalar.activation(v_listed[b, f][:], (v_second[b] if f else v_first)[:].indirect(listed(b)), ACT.Copy)
 
         def turn_v(b, tag):
             turned = psum.tile([P, 2, 2, P], F32, name="turned_v", tag=tag)
@@ -144,7 +145,7 @@ def tile_attend_soft_draft_segb2q256n512t2048_kernel(
             return turned
 
         def copy_v(b, turned):
-            vt[b] = reused.tile([P, DV, PACK], BF16, name=f"vt{b}", offset=V_AT + 8 * T + 4 * N * (b + 1), align_bytes=64)
+            vt[b] = reused.tile([P, DV, PACK], BF16, name=f"vt{b}", offset=V_AT + 10 * T + 4 * N * (QT + b), align_bytes=64)
             nc.scalar.copy(
                 vt[b][:].rearrange("s e t -> s (e t)").bitcast(F32).rearrange("s (f e u) -> s f e u", f=2, u=2),
                 turned[:].rearrange("s f u e -> s f e u"),
@@ -169,25 +170,22 @@ def tile_attend_soft_draft_segb2q256n512t2048_kernel(
             )
 
         def make_penalty(i):
-            nc.scalar.activation(
-                penalty[:, i],
-                pos_wide[i // QT][:].rearrange("q (s t) -> q t s", t=PACK),
-                ACT.Relu,
-                bias=qbias[:, i : i + 1],
-                scale=-1.0,
-            )
+            nc.scalar.activation(penalty[:, i], pos_wide[i // QT][:], ACT.Relu, bias=qbias[:, i : i + 1], scale=-1.0)
 
         def apply_mask(i):
-            negs[i] = reused.tile([P, PACK, P], F32, name=f"negs{i}", offset=V_AT + 8 * T + 4 * N * i)
-            nc.vector.scalar_tensor_tensor(
-                negs[i][:], penalty[:, i], PENALTY, score[i][:].rearrange("q (s t) -> q t s", t=PACK), ALU.min, ALU.subtract
-            )
+            negs[i] = reused.tile([P, N], F32, name=f"negs{i}", offset=V_AT + 10 * T + 4 * N * i)
+            nc.vector.scalar_tensor_tensor(negs[i][:], penalty[:, i], PENALTY, score[i][:], ALU.min, ALU.subtract)
 
         def weigh(i):
-            nc.vector.tensor_reduce(negm[i][:], negs[i][:].rearrange("q t s -> q (t s)"), AX.X, ALU.min)
+            nc.vector.tensor_reduce(negm[i][:], negs[i][:], AX.X, ALU.min)
             prob[i] = reused.tile([P, PACK, P], F32, name=f"prob{i}", offset=V_AT + 4 * T + 4 * N * i)
             nc.scalar.activation(
-                prob[i][:], negs[i][:], ACT.Exp, bias=negm[i][:], scale=-1.0, accum_out=totals[:, i : i + 1]
+                prob[i][:].rearrange("q t s -> q s t"),
+                negs[i][:].rearrange("q (s t) -> q s t", t=PACK),
+                ACT.Exp,
+                bias=negm[i][:],
+                scale=-1.0,
+                accum_out=totals[:, i : i + 1],
             )
 
         def turn_p(i, tag):
@@ -232,25 +230,22 @@ def tile_attend_soft_draft_segb2q256n512t2048_kernel(
                 nc.scalar.activation(y[:], acc[:, 0:DV], ACT.Copy, scale=invs[:, i : i + 1])
             nc.sync.dma_start(out[b, h * P : (h + 1) * P, :], y[:])
 
-        pos_turned = [turn_pos(b) for b in range(B)]
-        first = held.tile([P, QP_AT + 1], F32, name="first")
-        nc.scalar.mul(first[:], pos_turned[0][:, LIVE : QP_AT + P], -STRETCH)
-        qbias = first[:, QP_AT + 1 - TILES :]
-        widen_pos(0, first)
-        nc.vector.tensor_copy(ks[:], ks_pool[:].bitcast(U8).indirect(offsets[:]))
+        pos_turned = psum.tile([P, N], F32, name="turned", tag="turned")
+        nc.tensor.transpose(pos_turned[:, QP_AT : QP_AT + P], qp[:], ident[:])
         for b in range(B):
-            gather_kw(b)
-        for b in range(B):
-            gather_v(b, 0)
-        second = reused.tile([P, 2 * PACK], F32, name="second", offset=4 * TILES * N)
-        nc.scalar.mul(second[:, 0 : 2 * PACK - 1], pos_turned[1][:, LIVE : LIVE + 2 * PACK - 1], -STRETCH)
-        widen_pos(1, second)
+            turn_pos(b)
         deal_vs()
-        penalty = reused.tile([P, TILES, PACK, P], F32, name="penalty", offset=0)
+        nc.vector.tensor_copy(ks[:], ks_pool[:].bitcast(U8).indirect(offsets[:]))
+        places = reused.tile([P, QP_AT + 1], F32, name="places", offset=0)
+        nc.vector.tensor_scalar(places[:], pos_turned[:, LIVE : QP_AT + P], -STRETCH, None, ALU.mult)
+        qbias = places[:, QP_AT + 1 - TILES :]
+        for b in range(B):
+            widen_pos(b)
+            gather_kw(b)
+            gather_v(b, 0)
+        penalty = reused.tile([P, TILES, N], F32, name="penalty", offset=T)
         for i in range(TILES):
             make_penalty(i)
-        for b in range(B):
-            gather_v(b, 1)
 
         for i in range(QT):
             scores(i)
@@ -261,25 +256,27 @@ def tile_attend_soft_draft_segb2q256n512t2048_kernel(
         for i in range(QT):
             weigh(i)
             apply_mask(i + QT)
-        v_turned = [turn_v(b, "turned") for b in range(B)]
         turn_p(0, "probT")
         turn_p(1, "probT")
+        for b in range(B):
+            gather_v(b, 1)
+        v_turned = [turn_v(b, "score") for b in range(B)]
         weigh(2)
         weigh(3)
-        for b in range(B):
-            copy_v(b, v_turned[b])
-        turn_p(2, "score")
-        turn_p(3, "score")
+        turn_p(2, "turned")
+        turn_p(3, "turned")
 
+        copy_v(0, v_turned[0])
+        copy_v(1, v_turned[1])
         scale_w(0)
         scale_w(1)
         scale_w(2)
         quantize_w([0, 1], w_pair[:].rearrange("s i q t -> s (i q t)"))
-        nc.vector.reciprocal(invs[:], totals[:])
         scale_w(3)
         quantize_v(0)
-        for i in range(QT, TILES):
-            quantize_w([i], wT[i][:].rearrange("s q t -> s (q t)"))
+        nc.vector.reciprocal(invs[:], totals[:])
+        quantize_w([2], wT[2][:].rearrange("s q t -> s (q t)"))
         quantize_v(1)
+        quantize_w([3], wT[3][:].rearrange("s q t -> s (q t)"))
         for i in range(TILES):
             finish(i, "pos_wide" if i < QT else "probT")

@@ -27,8 +27,12 @@ CHUNKS = B * N // P
 LIVE = P - 1
 STRETCH = 2.0**80
 PENALTY = 2.0**50
-V_AT = 6 * 1024
-QP_AT = 20
+VS_AT = 6 * 4 * SEG
+ZERO_AT = 8 * 4 * SEG
+
+
+def v_at(b, f):
+    return 4 * SEG * (3 * f + b)
 
 
 def tile_attend_soft_draft_segb2q256n512t2048_kernel(
@@ -42,30 +46,41 @@ def tile_attend_soft_draft_segb2q256n512t2048_kernel(
 
         offsets = held.tile([P, B * COLS], U16, name="offsets")
         kw_pool = held.tile([P, T], U32, name="kw_pool")
-        ks_pool = reused.tile([P, T // 4], I32, name="ks_pool", offset=0)
+        ks_pool = held.tile([P, T // 4], I32, name="ks_pool")
         qw = held.tile([P, B, NQ], U32, name="qw", align_bytes=64)
         qs = held.tile([P, B * NQ // 4], I32, name="qs", align_bytes=64)
         pos_pool = held.tile([P, T], F32, name="pos_pool")
-        vs_pool = held.tile([P, T], F32, name="vs_pool")
+        vs_pool = reused.tile([P, T], F32, name="vs_pool", offset=VS_AT)
         qp = held.tile([P, P], F32, name="qp")
-        v_first = reused.tile([P, T], F32, name="v_first", offset=V_AT)
-        v_second = [
-            reused.tile([P, SEG], F32, name="v_second0", offset=V_AT + 4 * T),
-            reused.tile([P, T], F32, name="v_second1", offset=V_AT + 4 * T + 4 * SEG),
-        ]
+        v_pool = {
+            (b, f): reused.tile([P, (b + 1) * SEG], F32, name=f"v_pool{b}{f}", offset=v_at(b, f))
+            for f in range(2)
+            for b in range(B)
+        }
         ident = held.tile([P, P], F32, name="ident")
         negm = [held.tile([P, 1], F32, name=f"negm{i}") for i in range(TILES)]
         totals = held.tile([P, TILES], F32, name="totals")
         invs = held.tile([P, TILES], F32, name="invs")
 
-        nc.gpsimd.memset(ks_pool[:], 0)
-        nc.gpsimd.memset(qs[:], 0)
-        nc.gpsimd.memset(qp[0 : P - TILES, :], 0.0)
-        zero = held.tile([P, 1], F32, name="zero")
+        zero = reused.tile([P, 1], F32, name="zero", offset=ZERO_AT)
         nc.vector.memset(zero[:], 0.0)
+        nc.gpsimd.memset(ks_pool[:], 0)
         nc.vector.memset(pos_pool[0:LIVE, :], 0.0)
-        nc.vector.memset(vs_pool[0:LIVE, :], 0.0)
-        nc.vector.memset(v_second[1][:, 0:SEG], 0.0)
+        make_identity(nc, ident[:])
+        nc.gpsimd.memset(qs[:], 0)
+        nc.gpsimd.memset(v_pool[1, 0][:, 0:SEG], 0.0)
+        nc.gpsimd.memset(vs_pool[0:LIVE, :], 0.0)
+        nc.gpsimd.memset(v_pool[1, 1][:, 0:SEG], 0.0)
+
+        def own(b):
+            return slice(b * SEG, (b + 1) * SEG)
+
+        def load_kw(b):
+            words = k_words[0].rearrange("p n t -> p (n t)")
+            nc.sync.dma_start(kw_pool[:, own(b)].bitcast(I32), words[:, PACK * b * SEG : PACK * (b + 1) * SEG].bitcast(I32))
+
+        def load_v(b, f):
+            nc.sync.dma_start(v_pool[b, f][:, own(b)], vT[f * P : (f + 1) * P, own(b)])
 
         def load_ks(g):
             nc.sync.dma_start(ks_pool[32 * g : 32 * g + 4, :], k_scales[0, 4 * g : 4 * g + 4, :].bitcast(I32))
@@ -77,21 +92,21 @@ def tile_attend_soft_draft_segb2q256n512t2048_kernel(
             )
 
         nc.scalar.dma_start(pos_pool[LIVE:P, :], pos[0:1, :])
-        nc.scalar.activation(ident[:], zero[:].to_broadcast([P, P]), ACT.Copy)
-        make_identity(nc, ident[:], nomemset=True)
+        nc.scalar.activation(qp[0 : P - TILES, :], zero[0 : P - TILES, :].to_broadcast([P - TILES, P]), ACT.Copy)
         nc.sync.dma_start(offsets[:], offs)
-        nc.sync.dma_start(vs_pool[LIVE:P, :], vs[0:1, :])
+        load_kw(0)
         for g in range(4):
             load_ks(g)
-        nc.sync.dma_start(v_first[:], vT[0:P, :])
+        load_v(0, 0)
+        load_kw(1)
         nc.sync.dma_start(qp[P - TILES : P, :], qpos.rearrange("b (h p) o -> (b h) (p o)", p=P))
-        nc.sync.dma_start(kw_pool[:].bitcast(I32), k_words[0].rearrange("p n t -> p (n t)").bitcast(I32))
+        load_v(1, 0)
         nc.sync.dma_start(qw[:].bitcast(I32), q_words[:, 0].rearrange("b p q t -> p b (q t)").bitcast(I32))
         for g in range(4):
             load_qs(g)
+        nc.sync.dma_start(vs_pool[LIVE:P, :], vs[0:1, :])
         for b in range(B):
-            cols = slice(b * SEG, (b + 1) * SEG)
-            nc.sync.dma_start(v_second[b][:, cols], vT[P : 2 * P, cols])
+            load_v(b, 1)
 
         def listed(b):
             return offsets[:, b * COLS : (b + 1) * COLS]
@@ -133,8 +148,8 @@ def tile_attend_soft_draft_segb2q256n512t2048_kernel(
             nc.vector.tensor_copy(kw[b][:], kw_pool[:, window(b)].indirect(listed(b)))
 
         def gather_v(b, f):
-            v_listed[b, f] = held.tile([P, N], BF16, name=f"v_listed{b}{f}")
-            nc.scalar.activation(v_listed[b, f][:], (v_second[b] if f else v_first)[:].indirect(listed(b)), ACT.Copy)
+            v_listed[b, f] = reused.tile([P, N], BF16, name=f"v_listed{b}{f}", offset=ZERO_AT + 2 * N * ((b + 2 * f - 1) % 4))
+            nc.scalar.activation(v_listed[b, f][:], v_pool[b, f][:].indirect(listed(b)), ACT.Copy)
 
         def turn_v(b, tag):
             turned = psum.tile([P, 2, 2, P], F32, name="turned_v", tag=tag)
@@ -145,7 +160,7 @@ def tile_attend_soft_draft_segb2q256n512t2048_kernel(
             return turned
 
         def copy_v(b, turned):
-            vt[b] = reused.tile([P, DV, PACK], BF16, name=f"vt{b}", offset=V_AT + 10 * T + 4 * N * (QT + b), align_bytes=64)
+            vt[b] = reused.tile([P, DV, PACK], BF16, name=f"vt{b}", offset=VS_AT + 4 * N * (QT + b), align_bytes=64)
             nc.scalar.copy(
                 vt[b][:].rearrange("s e t -> s (e t)").bitcast(F32).rearrange("s (f e u) -> s f e u", f=2, u=2),
                 turned[:].rearrange("s f u e -> s f e u"),
@@ -173,12 +188,12 @@ def tile_attend_soft_draft_segb2q256n512t2048_kernel(
             nc.scalar.activation(penalty[:, i], pos_wide[i // QT][:], ACT.Relu, bias=qbias[:, i : i + 1], scale=-1.0)
 
         def apply_mask(i):
-            negs[i] = reused.tile([P, N], F32, name=f"negs{i}", offset=V_AT + 10 * T + 4 * N * i)
+            negs[i] = reused.tile([P, N], F32, name=f"negs{i}", offset=VS_AT + 4 * N * i)
             nc.vector.scalar_tensor_tensor(negs[i][:], penalty[:, i], PENALTY, score[i][:], ALU.min, ALU.subtract)
 
         def weigh(i):
             nc.vector.tensor_reduce(negm[i][:], negs[i][:], AX.X, ALU.min)
-            prob[i] = reused.tile([P, PACK, P], F32, name=f"prob{i}", offset=V_AT + 4 * T + 4 * N * i)
+            prob[i] = reused.tile([P, PACK, P], F32, name=f"prob{i}", offset=v_at(0, 1) + 4 * N * i)
             nc.scalar.activation(
                 prob[i][:].rearrange("q t s -> q s t"),
                 negs[i][:].rearrange("q (s t) -> q s t", t=PACK),
@@ -231,19 +246,25 @@ def tile_attend_soft_draft_segb2q256n512t2048_kernel(
             nc.sync.dma_start(out[b, h * P : (h + 1) * P, :], y[:])
 
         pos_turned = psum.tile([P, N], F32, name="turned", tag="turned")
-        nc.tensor.transpose(pos_turned[:, QP_AT : QP_AT + P], qp[:], ident[:])
         for b in range(B):
             turn_pos(b)
-        deal_vs()
+        gather_kw(0)
         nc.vector.tensor_copy(ks[:], ks_pool[:].bitcast(U8).indirect(offsets[:]))
-        places = reused.tile([P, QP_AT + 1], F32, name="places", offset=0)
-        nc.vector.tensor_scalar(places[:], pos_turned[:, LIVE : QP_AT + P], -STRETCH, None, ALU.mult)
-        qbias = places[:, QP_AT + 1 - TILES :]
+        gather_kw(1)
+        deal_vs()
+        gather_v(0, 0)
+        places = reused.tile([P, 2 * CHUNKS - 1], F32, name="places", offset=v_at(0, 0))
+        nc.scalar.activation(
+            places[:], pos_turned[:, LIVE : LIVE + 2 * CHUNKS - 1], ACT.Identity, bias=zero[:], scale=-STRETCH
+        )
         for b in range(B):
             widen_pos(b)
-            gather_kw(b)
-            gather_v(b, 0)
-        penalty = reused.tile([P, TILES, N], F32, name="penalty", offset=T)
+        qp_turned = psum.tile([P, P], F32, name="qp_turned", tag="turned")
+        nc.tensor.transpose(qp_turned[:], qp[:], ident[:])
+        qbias = reused.tile([P, TILES], F32, name="qbias", offset=v_at(0, 1) - 32)
+        gather_v(1, 0)
+        nc.scalar.mul(qbias[:], qp_turned[:, P - TILES : P], -STRETCH)
+        penalty = reused.tile([P, TILES, N], F32, name="penalty", offset=v_at(1, 0) - 4 * N)
         for i in range(TILES):
             make_penalty(i)
 

from contextlib import ExitStack

import concourse.mybir as mybir
from concourse.masks import make_identity

B, N, T, D, DV, NQ = 2, 512, 2048, 512, 256, 256
FLOPS = 2 * B * NQ * N * (D + DV)

F32 = mybir.dt.float32
BF16 = mybir.dt.bfloat16
I32 = mybir.dt.int32
U32 = mybir.dt.uint32
U16 = mybir.dt.uint16
U8 = mybir.dt.uint8
FP8X4 = mybir.dt.float8_e4m3fn_x4
ALU = mybir.AluOpType
ACT = mybir.ActivationFunctionType
AX = mybir.AxisListType

P = 128
PACK = 4
SEG = T // B
COLS = N // 16
QT = NQ // P
TILES = B * QT
CHUNKS = B * N // P
LIVE = P - 1
STRETCH = 2.0**80
PENALTY = 2.0**50
VS_AT = 6 * 4 * SEG
ZERO_AT = 8 * 4 * SEG


def v_at(b, f):
    return 4 * SEG * (3 * f + b)


def tile_attend_soft_draft_segb2q256n512t2048_kernel(
    tc, q_words, q_scales, k_words, k_scales, vT, vs, pos, qpos, offs, out
):
    nc = tc.nc
    with ExitStack() as ctx:
        held = ctx.enter_context(tc.tile_pool(name="held", bufs=1))
        reused = ctx.enter_context(tc.tile_pool(name="reused", bufs=1))
        psum = ctx.enter_context(tc.psum_pool(name="psum", bufs=2))

        offsets = held.tile([P, B * COLS], U16, name="offsets")
        kw_pool = held.tile([P, T], U32, name="kw_pool")
        ks_pool = held.tile([P, T // 4], I32, name="ks_pool")
        qw = held.tile([P, B, NQ], U32, name="qw", align_bytes=64)
        qs = held.tile([P, B * NQ // 4], I32, name="qs", align_bytes=64)
        pos_pool = held.tile([P, T], F32, name="pos_pool")
        vs_pool = reused.tile([P, T], F32, name="vs_pool", offset=VS_AT)
        qp = held.tile([P, P], F32, name="qp")
        v_pool = {
            (b, f): reused.tile([P, (b + 1) * SEG], F32, name=f"v_pool{b}{f}", offset=v_at(b, f))
            for f in range(2)
            for b in range(B)
        }
        ident = held.tile([P, P], F32, name="ident")
        negm = [held.tile([P, 1], F32, name=f"negm{i}") for i in range(TILES)]
        totals = held.tile([P, TILES], F32, name="totals")
        invs = held.tile([P, TILES], F32, name="invs")

        zero = reused.tile([P, 1], F32, name="zero", offset=ZERO_AT)
        nc.vector.memset(zero[:], 0.0)
        nc.gpsimd.memset(ks_pool[:], 0)
        nc.vector.memset(pos_pool[0:LIVE, :], 0.0)
        make_identity(nc, ident[:])
        nc.gpsimd.memset(qs[:], 0)
        nc.gpsimd.memset(v_pool[1, 0][:, 0:SEG], 0.0)
        nc.gpsimd.memset(vs_pool[0:LIVE, :], 0.0)
        nc.gpsimd.memset(v_pool[1, 1][:, 0:SEG], 0.0)

        def own(b):
            return slice(b * SEG, (b + 1) * SEG)

        def load_kw(b):
            words = k_words[0].rearrange("p n t -> p (n t)")
            nc.sync.dma_start(kw_pool[:, own(b)].bitcast(I32), words[:, PACK * b * SEG : PACK * (b + 1) * SEG].bitcast(I32))

        def load_v(b, f):
            nc.sync.dma_start(v_pool[b, f][:, own(b)], vT[f * P : (f + 1) * P, own(b)])

        def load_ks(g):
            nc.sync.dma_start(ks_pool[32 * g : 32 * g + 4, :], k_scales[0, 4 * g : 4 * g + 4, :].bitcast(I32))

        def load_qs(g):
            nc.sync.dma_start(
                qs[32 * g : 32 * g + 4, :].rearrange("p (b c) -> p b c", b=B),
                q_scales[:, 0, 4 * g : 4 * g + 4, :].rearrange("b f q -> f b q").bitcast(I32),
            )

        nc.scalar.dma_start(pos_pool[LIVE:P, :], pos[0:1, :])
        nc.scalar.activation(qp[0 : P - TILES, :], zero[0 : P - TILES, :].to_broadcast([P - TILES, P]), ACT.Copy)
        nc.sync.dma_start(offsets[:], offs)
        load_kw(0)
        for g in range(4):
            load_ks(g)
        load_v(0, 0)
        load_kw(1)
        nc.sync.dma_start(qp[P - TILES : P, :], qpos.rearrange("b (h p) o -> (b h) (p o)", p=P))
        load_v(1, 0)
        nc.sync.dma_start(qw[:].bitcast(I32), q_words[:, 0].rearrange("b p q t -> p b (q t)").bitcast(I32))
        for g in range(4):
            load_qs(g)
        nc.sync.dma_start(vs_pool[LIVE:P, :], vs[0:1, :])
        for b in range(B):
            load_v(b, 1)

        def listed(b):
            return offsets[:, b * COLS : (b + 1) * COLS]

        def window(b):
            return slice(0, (b + 1) * SEG)

        kw, pos_wide, v_listed = {}, {}, {}
        score, negs, prob, probT, wT, wq, wsc = {}, {}, {}, {}, {}, {}, {}
        ks = held.tile([P, B * N], U8, name="ks", align_bytes=64)
        vt, vq, vsc = {}, {}, {}
        vs_col = [held.tile([P, PACK], F32, name=f"vs_col{b}") for b in range(B)]
        w_pair = held.tile([P, QT, P, PACK], BF16, name="w_pair", align_bytes=64)

        def turn_pos(b):
            row = held.tile([P, N], F32, name=f"pos_row{b}")
            nc.scalar.activation(row[:], pos_pool[:, window(b)].indirect(listed(b)), ACT.Copy)
            for c in range(N // P):
                at = LIVE + place(b, c) - (P - 1)
                nc.tensor.transpose(pos_turned[:, at : at + P], row[:, c * P : (c + 1) * P], ident[:])

        def place(b, c):
            return 2 * (CHUNKS - 1 - b * (N // P) - c)

        def widen_pos(b):
            pos_wide[b] = psum.tile([P, N], F32, name="pos_wide", tag="pos_wide")
            for c in range(N // P):
                column = places[:, place(b, c) : place(b, c) + 1]
                nc.tensor.transpose(pos_wide[b][:, c * P : (c + 1) * P], column.to_broadcast([P, P]), ident[:])

        def deal_vs():
            row = held.tile([P, B * N], F32, name="vs_row")
            nc.vector.tensor_copy(row[:], vs_pool[:].indirect(offsets[:]))
            for b in range(B):
                nc.sync.dma_start(vs_col[b][:], row[LIVE:P, b * N : (b + 1) * N])

        def gather_kw(b):
            kw[b] = held.tile([P, N], U32, name=f"kw{b}", align_bytes=64)
            nc.vector.tensor_copy(kw[b][:], kw_pool[:, window(b)].indirect(listed(b)))

        def gather_v(b, f):
            v_listed[b, f] = reused.tile([P, N], BF16, name=f"v_listed{b}{f}", offset=ZERO_AT + 2 * N * ((b + 2 * f - 1) % 4))
            nc.scalar.activation(v_listed[b, f][:], v_pool[b, f][:].indirect(listed(b)), ACT.Copy)

        def turn_v(b, tag):
            turned = psum.tile([P, 2, 2, P], F32, name="turned_v", tag=tag)
            for f in range(2):
                pairs = v_listed[b, f][:].bitcast(F32)
                for u in range(2):
                    nc.tensor.transpose(turned[:, f, u, :], pairs[:, u : 2 * P : 2], ident[:])
            return turned

        def copy_v(b, turned):
            vt[b] = reused.tile([P, DV, PACK], BF16, name=f"vt{b}", offset=VS_AT + 4 * N * (QT + b), align_bytes=64)
            nc.scalar.copy(
                vt[b][:].rearrange("s e t -> s (e t)").bitcast(F32).rearrange("s (f e u) -> s f e u", f=2, u=2),
                turned[:].rearrange("s f u e -> s f e u"),
            )

        def quantize_v(b):
            vq[b] = held.tile([P, DV], U32, name=f"vq{b}", align_bytes=64)
            vsc[b] = held.tile([P, DV], U8, name=f"vsc{b}", align_bytes=64)
            nc.vector.quantize_mx(vq[b][:].bitcast(FP8X4), vsc[b][:], vt[b][:].rearrange("s e t -> s (e t)"))

        def scores(i):
            b, h = divmod(i, QT)
            score[i] = psum.tile([P, N], F32, name="score", tag="score")
            nc.tensor.matmul_mx(
                score[i][:],
                lhsT=qw[:, b, h * P : (h + 1) * P].bitcast(FP8X4),
                lhsT_scale=qs[:].bitcast(U8)[:, i * P : (i + 1) * P],
                rhs=kw[b][:].bitcast(FP8X4),
                rhs_scale=ks[:, b * N : (b + 1) * N],
                start=True,
                stop=True,
            )

        def make_penalty(i):
            nc.scalar.activation(penalty[:, i], pos_wide[i // QT][:], ACT.Relu, bias=qbias[:, i : i + 1], scale=-1.0)

        def apply_mask(i):
            negs[i] = reused.tile([P, N], F32, name=f"negs{i}", offset=VS_AT + 4 * N * i)
            nc.vector.scalar_tensor_tensor(negs[i][:], penalty[:, i], PENALTY, score[i][:], ALU.min, ALU.subtract)

        def weigh(i):
            nc.vector.tensor_reduce(negm[i][:], negs[i][:], AX.X, ALU.min)
            prob[i] = reused.tile([P, PACK, P], F32, name=f"prob{i}", offset=v_at(0, 1) + 4 * N * i)
            nc.scalar.activation(
                prob[i][:].rearrange("q t s -> q s t"),
                negs[i][:].rearrange("q (s t) -> q s t", t=PACK),
                ACT.Exp,
                bias=negm[i][:],
                scale=-1.0,
                accum_out=totals[:, i : i + 1],
            )

        def turn_p(i, tag):
            probT[i] = psum.tile([P, PACK, P], F32, name="probT", tag=tag)
            for t in range(PACK):
                nc.tensor.transpose(probT[i][:, t, :], prob[i][:, t, :], ident[:])

        def scale_w(i):
            b = i // QT
            wT[i] = w_pair[:, i] if b == 0 else held.tile([P, P, PACK], BF16, name=f"wT{i}", align_bytes=64)
            nc.vector.tensor_tensor(
                wT[i][:],
                probT[i][:].rearrange("s t q -> s q t"),
                vs_col[b][:].unsqueeze(1).to_broadcast([P, P, PACK]),
                ALU.mult,
            )

        def quantize_w(tiles, values):
            codes = held.tile([P, len(tiles) * P], U32, name=f"wq{tiles[0]}", align_bytes=64)
            scales = held.tile([P, len(tiles) * P], U8, name=f"wsc{tiles[0]}", align_bytes=64)
            nc.vector.quantize_mx(codes[:].bitcast(FP8X4), scales[:], values)
            for n, i in enumerate(tiles):
                wq[i] = codes[:, n * P : (n + 1) * P]
                wsc[i] = scales[:, n * P : (n + 1) * P]

        def finish(i, tag):
            b, h = divmod(i, QT)
            acc = psum.tile([P, N], F32, name="acc", tag=tag)
            nc.tensor.matmul_mx(
                acc[:, 0:DV],
                lhsT=wq[i].bitcast(FP8X4),
                lhsT_scale=wsc[i],
                rhs=vq[b][:].bitcast(FP8X4),
                rhs_scale=vsc[b][:],
                start=True,
                stop=True,
            )
            y = held.tile([P, DV], F32, name=f"y{i}")
            if i == TILES - 1:
                nc.vector.tensor_scalar(y[:], acc[:, 0:DV], invs[:, i : i + 1], None, ALU.mult)
            else:
                nc.scalar.activation(y[:], acc[:, 0:DV], ACT.Copy, scale=invs[:, i : i + 1])
            nc.sync.dma_start(out[b, h * P : (h + 1) * P, :], y[:])

        pos_turned = psum.tile([P, N], F32, name="turned", tag="turned")
        for b in range(B):
            turn_pos(b)
        gather_kw(0)
        nc.vector.tensor_copy(ks[:], ks_pool[:].bitcast(U8).indirect(offsets[:]))
        gather_kw(1)
        deal_vs()
        gather_v(0, 0)
        places = reused.tile([P, 2 * CHUNKS - 1], F32, name="places", offset=v_at(0, 0))
        nc.scalar.activation(
            places[:], pos_turned[:, LIVE : LIVE + 2 * CHUNKS - 1], ACT.Identity, bias=zero[:], scale=-STRETCH
        )
        for b in range(B):
            widen_pos(b)
        qp_turned = psum.tile([P, P], F32, name="qp_turned", tag="turned")
        nc.tensor.transpose(qp_turned[:], qp[:], ident[:])
        qbias = reused.tile([P, TILES], F32, name="qbias", offset=v_at(0, 1) - 32)
        gather_v(1, 0)
        nc.scalar.mul(qbias[:], qp_turned[:, P - TILES : P], -STRETCH)
        penalty = reused.tile([P, TILES, N], F32, name="penalty", offset=v_at(1, 0) - 4 * N)
        for i in range(TILES):
            make_penalty(i)

        for i in range(QT):
            scores(i)
        for i in range(QT):
            apply_mask(i)
        for i in range(QT, TILES):
            scores(i)
        for i in range(QT):
            weigh(i)
            apply_mask(i + QT)
        turn_p(0, "probT")
        turn_p(1, "probT")
        for b in range(B):
            gather_v(b, 1)
        v_turned = [turn_v(b, "score") for b in range(B)]
        weigh(2)
        weigh(3)
        turn_p(2, "turned")
        turn_p(3, "turned")

        copy_v(0, v_turned[0])
        copy_v(1, v_turned[1])
        scale_w(0)
        scale_w(1)
        scale_w(2)
        quantize_w([0, 1], w_pair[:].rearrange("s i q t -> s (i q t)"))
        scale_w(3)
        quantize_v(0)
        nc.vector.reciprocal(invs[:], totals[:])
        quantize_w([2], wT[2][:].rearrange("s q t -> s (q t)"))
        quantize_v(1)
        quantize_w([3], wT[3][:].rearrange("s q t -> s (q t)"))
        for i in range(TILES):
            finish(i, "pos_wide" if i < QT else "probT")
